import numpy as np, ml_dtypes
CORES = [23,119,17,113]
N = 4
BF = ml_dtypes.bfloat16
def gentries(a):
    return np.ascontiguousarray(a.reshape(8, 16, -1).transpose(0, 2, 1)).reshape(8, -1)
def gtable(e):
    e = np.asarray(e); return np.ascontiguousarray(e.reshape(8, -1, 16).transpose(0, 2, 1)).reshape(128, -1).astype(np.int32)
V, B, L = 2048, 128, 3
W = V + (N - 1) * B
def parts(rng):
    x = (3 * rng.integers(0, 256, (N, 8, 1, V)) + rng.integers(0, 256, (N, 8, 16, V)) + rng.integers(0, 2, (N, 8, 16, V))) >> 2
    t = rng.integers(1, 97, (N, 8, 16, 1)); nx = np.argsort(rng.random((N, 8, 2 * W)), axis=-1)
    sh = np.argsort(rng.random((N, 8, N - 1, V)), axis=-1)[..., :B]
    return np.minimum(x, 255), t, np.ascontiguousarray(nx), np.ascontiguousarray(sh)
def both(rng, a):
    w = rng.integers(0, 2, (len(a), 1)); return 2 * a[:, None] + np.concatenate([w, 1 - w], axis=1)
def chains(rng, g, x, t, nx, sh):
    K = min(B, (V - B) // (3 * N) // 32 * 32); n = N * K
    t[:, g] = 256 * (N - 1) + 1; o = np.argsort(rng.random((N, N - 1, B)), axis=2)
    s = np.stack([3 * n + rng.permutation(V - 3 * n)[:B] for q in range(N)])
    for q in range(N):
        sh[q, g] = s[q][o[q]]
    for r in range(N):
        u = np.concatenate([s[r, :K]] + [V + (d - 1) * B + np.flatnonzero(o[(r - d) % N, d - 1] < K) for d in range(1, N)])
        m = rng.permutation(2 * n); a = m[:n]; e = m[n:]; b = 2 * n + rng.permutation(n)
        x[r, g][:, m] = 0; x[r, g][:, b] = 255; x[r, g][:, s[r, :K]] = 255
        nx[r, g] = np.arange(2 * W)
        for i, j in ((u, a), (a, b), (b, e), (e, u)):
            w = rng.integers(0, 2, n); nx[r, g, 2 * i] = 2 * j + w; nx[r, g, 2 * i + 1] = 2 * j + 1 - w
def put(rng, y, p, nodes, order, high):
    v = rng.integers(0, 4, (4, len(nodes))); y[:, nodes] = order; y[np.ix_(p, nodes)] = 255 - v if high else v
def swell(rng, g, x, t, nx, sh):
    K = 32; n = N * K; m = N * 8; lo = 4 * n
    p = rng.permutation(16)[:4]; t[:, g, p[:2]] = 4095; t[:, g, p[2]] = 0; t[:, g, p[3]] = 301
    o = np.argsort(rng.random((N, N - 1, B)), axis=2); s = np.stack([lo + rng.permutation(V - lo)[:B] for q in range(N)]); one = int(rng.integers(0, N))
    for q in range(N):
        sh[q, g] = s[q][o[q]]
    for r in range(N):
        u = rng.permutation(np.concatenate([s[r, :K]] + [V + (d - 1) * B + np.flatnonzero(o[(r - d) % N, d - 1] < K) for d in range(1, N)]))
        w = rng.permutation(lo); v = x[r, g]; y = nx[r, g]; y[:] = np.arange(2 * W); put(rng, v, p, s[r, :K], 0, True)
        if r != one:
            a = w[:n]; e = w[n:2 * n]; b = w[2 * n:3 * n]
            put(rng, v, p, w[:2 * n], 127, False); put(rng, v, p, b, 254, True)
            for i, j in ((u, a), (a, b), (b, e), (e, u)):
                y[both(rng, i)] = both(rng, j)
        else:
            c = w[:m]; zh = w[m:2 * m]; zl = w[2 * m:3 * m]; f1 = w[3 * m:5 * m]; f2 = w[5 * m:7 * m]; a1 = w[7 * m:10 * m]; a2 = w[10 * m:13 * m]; b = w[13 * m:16 * m]
            for i, k, h in ((c, 254, True), (zh, 254, False), (zl, 0, False), (f1, 127, True), (f2, 127, True), (a1, 127, False), (a2, 127, False), (b, 254, True)):
                put(rng, v, p, i, k, h)
            ui = both(rng, u); uo = both(rng, u)
            i = both(rng, f1); j = both(rng, f1)
            y[both(rng, c).ravel()] = i[:, 0]; y[both(rng, zh).ravel()] = i[:, 1]; y[j[:, 0]] = ui[:2 * m, 0]; y[j[:, 1]] = both(rng, zl).ravel()
            i = both(rng, f2); j = both(rng, f2)
            y[uo[2 * m:, 0]] = i[:, 0]; y[both(rng, zl).ravel()] = i[:, 1]; y[j[:, 0]] = both(rng, c).ravel(); y[j[:, 1]] = both(rng, zh).ravel()
            i = np.concatenate([ui[:2 * m, 1], ui[2 * m:].ravel()]); j = np.concatenate([uo[:2 * m].ravel(), uo[2 * m:, 1]])
            y[both(rng, b).ravel()] = rng.permutation(both(rng, a1).ravel()); y[both(rng, a1).ravel()] = rng.permutation(i)
            y[j] = rng.permutation(both(rng, a2).ravel()); y[both(rng, a2).ravel()] = rng.permutation(both(rng, b).ravel())
def crowd(rng, g, x, nx, sh, two):
    k = W // 5 if two else W // 2; lo = 3 * k if two else k
    x[:, g] = rng.integers(0, 256, (16, 1))
    for q in range(N):
        s = lo + rng.permutation(V - lo)[:B]; y = nx[q, g]; y[:] = np.arange(2 * W)
        for d in range(N - 1): sh[q, g, d] = rng.permutation(s)
        if two:
            ab = k + rng.permutation(2 * k); ce = 3 * k + rng.permutation(2 * k); five = (rng.permutation(k), ab[:k], ab[k:], ce[:k], ce[k:])
            om, oa, ob, oc, oe = [both(rng, z) for z in five]; im, ia, ib, ic, ie = [both(rng, z) for z in five]
            y[oa[:, 0]] = im[:, 0]; y[oa[:, 1]] = ic[:, 1]; y[ob[:, 0]] = im[:, 1]; y[ob[:, 1]] = ie[:, 1]; y[om[:, 0]] = ic[:, 0]; y[om[:, 1]] = ie[:, 0]
            y[oc[:, 0]] = ia[:, 0]; y[oc[:, 1]] = ib[:, 0]; y[oe[:, 0]] = ia[:, 1]; y[oe[:, 1]] = ib[:, 1]
        else:
            a = rng.permutation(k); b = k + rng.permutation(k)
            y[both(rng, a)] = both(rng, b); y[both(rng, b)] = both(rng, a)
def pack(x, t, nx, sh):
    return {"x0": np.ascontiguousarray(x.reshape(N, 128, V)).astype(np.int32), "th": np.ascontiguousarray(t.reshape(N, 128, 1)).astype(np.int32),
            "nxt": np.stack([gtable(a) for a in nx]), "shw": np.stack([gtable(a.reshape(8, -1)) for a in sh])}
def setup_inputs(rng):
    return pack(*parts(rng))
def setup_inputs_flat(rng):
    x, t, nx, sh = parts(rng)
    x[:, 0] = 255; x[:, 2] = rng.integers(0, 2, (N, 16, V)); x[:, 3] = 255 * rng.integers(0, 2, (N, 16, V))
    x[:, 4] = 255 * rng.integers(0, 2, (N, 1, V)); x[:, 5] = rng.integers(0, 4, (N, 1, V)); x[:, 6] = 64 * rng.integers(0, 4, (N, 16, V))
    v = np.array([0, 1, 2, 63, 64, 65, 127, 128, 129, 191, 192, 255, 256])
    t[:, ::2] = rng.choice(v, (N, 4, 16, 1)); t[:, 3] = rng.choice(v, (N, 16, 1)); t[:, 5] = rng.choice(np.array([0, 1, 2, 3]), (N, 16, 1))
    crowd(rng, 1, x, nx, sh, True); crowd(rng, 7, x, nx, sh, False)
    return pack(x, t, nx, sh)
def setup_inputs_loops(rng):
    x, t, nx, sh = parts(rng); p = np.arange(2 * W)
    for q in range(N):
        nx[q, 1] = p; nx[q, 2] = (p ^ 2) ^ np.repeat(rng.integers(0, 2, W), 2)
        nx[q, 3] = (p + 2) % (2 * W); nx[q, 5] = np.where(p & 1 == 0, (p + 2) % (2 * W), (p - 2) % (2 * W))
        i = np.flatnonzero(rng.random(2 * W) < 0.5); nx[q, 6] = p; nx[q, 6, i] = rng.permutation(i)
    chains(rng, 0, x, t, nx, sh); chains(rng, 4, x, t, nx, sh); swell(rng, 7, x, t, nx, sh)
    return pack(x, t, nx, sh)
def setup_inputs_ends(rng):
    x, t, nx, sh = parts(rng); k = 2 * (N - 1) * B
    for q in range(N):
        for g in range(8):
            if g % 2 == 0:
                s = np.concatenate([np.array([0, V - 1]), 1 + rng.permutation(V - 2)[:B - 2]])
                for d in range(N - 1): sh[q, g, d] = rng.permutation(s)
            else:
                sh[q, g] = V - 1 - np.arange((N - 1) * B).reshape(N - 1, B)
            if g in (0, 3, 4):
                o = rng.permutation(2 * V); nx[q, g, 2 * V:] = o[:k]
                nx[q, g, :2 * V] = rng.permutation(np.concatenate([o[k:], np.arange(2 * V, 2 * W)]))
            if g == 5:
                nx[q, g] = np.concatenate([rng.permutation(2 * V), 2 * V + rng.permutation(k)])
    return pack(x, t, nx, sh)
def setup_inputs_uneven(rng):
    x, t, nx, sh = parts(rng); q = rng.permutation(N)
    x[q[0]] = rng.integers(0, 4, (8, 16, V)); t[q[1]] = 4095; t[q[2]] = 0; x[q[3]] = 255 * rng.integers(0, 2, (8, 16, V))
    return pack(x, t, nx, sh)
def setup_inputs_spread(rng):
    x, t, nx, sh = parts(rng)
    x = np.minimum((np.exp2(8 * rng.random((N, 8, 1, V))) * rng.random((N, 8, 16, V))).astype(np.int64), 255)
    t = np.minimum(np.exp2(12 * rng.random((N, 8, 16, 1))).astype(np.int64) - 1, 4095)
    return pack(x, t, nx, sh)
def check_inputs(d):
    bad = []
    for k, lo, hi in (("x0", 0, 255), ("th", 0, 4095), ("nxt", 0, 2 * W - 1), ("shw", 0, V - 1)):
        if np.min(d[k]) < lo or np.max(d[k]) > hi: bad.append("range of " + k)
    if any(np.any(np.sort(gentries(a), axis=1) != np.arange(2 * W)) for a in d["nxt"]): bad.append("nxt holds each number once")
    s = np.sort(np.stack([gentries(a) for a in d["shw"]]).reshape(N, 8, N - 1, B), axis=3)
    if np.any(s[..., 1:] == s[..., :-1]): bad.append("different nodes in a block of shw")
    return bad
def reference(x0, th, nxt, shw):
    x = np.zeros((N, 8, 16, W), np.int32); x[..., :V] = x0.reshape(N, 8, 16, V); t = th.astype(np.int32).reshape(N, 8, 16, 1)
    nx = np.stack([gentries(a) for a in nxt]).astype(np.int64); pv = np.argsort(nx, axis=2)
    sh = np.stack([gentries(a) for a in shw]).astype(np.int64).reshape(N, 8, N - 1, B)
    border = np.zeros((N, 8, V), bool); np.put_along_axis(border, sh.reshape(N, 8, -1), True, 2)
    may = np.zeros((N, 8, W), bool); may[..., :V] = ~border
    inn = np.ones((N, 8, W), bool); port = np.arange(2 * W)
    def pick(a, ports):
        return np.take_along_axis(a, (ports >> 1)[:, :, None, :], 3)
    def sum4(a, n, p):
        b = pick(a, p) + pick(a, n); return b[..., 0::2] + b[..., 1::2]
    def size(u):
        return np.add.reduce(np.minimum(np.abs(u), 255), axis=2)
    def outward(a):
        for r in range(N):
            for d in range(1, N):
                q = (r - d) % N
                a[r, :, :, V + (d - 1) * B:V + d * B] = np.take_along_axis(a[q], sh[q, :, d - 1][:, None, :], 2)
    def home(s):
        o = s[..., :V].copy()
        for r in range(N):
            for d in range(1, N):
                q = (r - d) % N; ix = sh[q, :, d - 1][:, None, :]
                np.put_along_axis(o[q], ix, np.take_along_axis(o[q], ix, 2) + s[r, :, :, V + (d - 1) * B:V + d * B], 2)
        return o
    det = np.zeros((N, 8, 16, W), np.int32); kept = []
    for lev in range(L):
        outward(x)
        a = pick(x, pv); b = pick(x, nx); a0, a1, b0, b1 = a[..., 0::2], a[..., 1::2], b[..., 0::2], b[..., 1::2]
        d = x - ((a0 + a1 + b0 + b1) >> 2)
        key = size(d).astype(np.int64) * 4096 + np.arange(W)
        k = np.minimum(np.take_along_axis(key, pv >> 1, 2), np.take_along_axis(key, nx >> 1, 2))
        lv = may & (key < np.minimum(k[..., 0::2], k[..., 1::2]))
        c = size(a0 - b1) + size(a1 - b0) < size(a0 - b0) + size(a1 - b1)
        s = np.where(lv[:, :, None, :], d >> 2, 0).astype(np.int32)
        x[..., :V] += home(sum4(s, nx, pv)) * inn[:, :, None, :V]
        det = np.where(lv[:, :, None, :], d, det); kept.append((lv, nx, pv, inn))
        l2 = np.repeat(lv, 2, axis=2); other = port ^ np.repeat(c, 2, axis=2).astype(np.int64)
        fn = np.where(l2, np.take_along_axis(nx, other, 2), port); fp = np.where(l2, np.take_along_axis(pv, other, 2), port)
        nx = np.take_along_axis(fn, nx, 2); pv = np.take_along_axis(fp, pv, 2)
        may = may & ~lv; inn = inn & ~lv
    det = np.where(np.abs(det) < t, 0, det).astype(np.int32)
    for lv, n, p, was in kept[::-1]:
        s = np.where(lv[:, :, None, :], det >> 2, 0).astype(np.int32)
        x[..., :V] -= home(sum4(s, n, p)) * was[:, :, None, :V]
        outward(x)
        x = np.where(lv[:, :, None, :], det + (sum4(x, n, p) >> 2), x).astype(np.int32)
    return {"yx": np.ascontiguousarray(x[..., :V]).reshape(N, 128, V).astype(np.float32), "yn": nx.astype(np.float32)}

@@ -1,0 +1,688 @@
+from concourse.bass import DstId, RemoteDMATransfer
+from concourse.mybir import AluOpType as OP, ActivationFunctionType as AF
+
+V, B, W, P2 = 2048, 128, 2432, 4864
+GH = 384
+MG = 12582912.0
+KP = 4096.0
+BIG = 1048576.0
+
+SCRATCH = {}
+for _n, _c, _t in (
+        ("xa", W, "float32"), ("key", W, "float32"), ("dd", V, "float32"), ("ad", V, "float32"),
+        ("sp1", V, "float32"), ("sp2", V, "float32"), ("dl1", V, "bfloat16"), ("dl2", V, "float32"),
+        ("ga", 4096, "float16"), ("gb", 4096, "float16"), ("fnx", P2, "bfloat16"), ("fpv", P2, "bfloat16"),
+        ("nxh", P2, "bfloat16"), ("pvh", P2, "bfloat16"), ("phl", P2, "bfloat16"), ("ghl", 768, "bfloat16"),
+        ("lv1", V, "bfloat16"), ("lv2", V, "bfloat16"), ("lv3", V, "bfloat16"), ("nm", V, "bfloat16"),
+        ("q0", 1024, "float32"), ("q1", 1024, "float32"),
+        ("unh", 2048, "bfloat16"), ("unl", 2048, "bfloat16"), ("wrp", 2048, "bfloat16"),
+        ("rdp", 1024, "bfloat16"), ("rdn", 1024, "bfloat16"),
+        ("idn", 128, "bfloat16"), ("neg", 128, "bfloat16"), ("ngq", 128, "bfloat16"), ("d25", 128, "bfloat16"),
+        ("blk", 128, "bfloat16"), ("blp", 128, "bfloat16"), ("bln", 128, "bfloat16"), ("sel", 128, "bfloat16"),
+        ("idh", 128, "float16"), ("neh", 128, "float16"), ("nqh", 128, "float16"), ("qr", 128, "bfloat16"),
+        ("swp", 128, "float32"), ("one", 1024, "bfloat16"),
+        ("x0i", 2380, "int32"), ("pci", 8, "int32"), ("col", 16, "float32"), ("th32", 8, "float32"), ("ls", 24, "uint16"),
+        ("pid", 304, "float32"), ("nxf", 304, "float32"), ("pvf", 304, "float32"),
+        ("dnn", 256, "float32"), ("dnp", 256, "float32"), ("dpn", 256, "float32"), ("dpp", 256, "float32"),
+        ("lw", 256, "float32"), ("lc", 256, "float32"), ("w0", 256, "float32"), ("w1", 256, "float32"),
+        ("hn", 256, "bfloat16"), ("hp", 256, "bfloat16"), ("ln_", 256, "bfloat16"), ("lp_", 256, "bfloat16"),
+        ("lpn", 304, "uint16"), ("lpp", 304, "uint16"),
+        ("sx", GH, "float32"), ("ss", 768, "float32"), ("rs1", 768, "float32"), ("rs2", 768, "float32"),
+        ("bs", 3 * GH, "float32"), ("rb1", GH, "float32"), ("rb2", GH, "float32"),
+        ("sg1", GH, "float32"), ("sg2", GH, "float32"), ("bt", 128, "float32")):
+    SCRATCH[_n] = ("sbuf", [128, _c], _t)
+NF, NT = 4, 6
+for _k in range(NF):
+    SCRATCH["f%d" % _k] = ("sbuf", [128, 512], "float32")
+for _k in range(NT):
+    SCRATCH["t%d" % _k] = ("sbuf", [128, 512], "bfloat16")
+for _k in range(8):
+    SCRATCH["p%d" % _k] = ("psum", [128, 512], "float32")
+for _k in (1, 2, 3):
+    SCRATCH["l%dn" % _k] = ("sbuf", [128, 304], "uint16")
+    SCRATCH["l%dp" % _k] = ("sbuf", [128, 304], "uint16")
+ARR = [a + str(d) for a in ("ax1_", "ax2_", "ax3_", "as1_", "as2_", "as3_", "ab3_", "ab2_") for d in (1, 2, 3)]
+SEMAPHORES = ["sv", "ss_", "st", "sg", "loc"] + ARR + ["d%d" % k for k in range(20)]
+PSUMS = ["p%d" % k for k in range(8)]
+CY = 0.00104
+WK = 0.1
+
+
+def R(name, a, b, s=1):
+    return (name, a, b, s)
+
+
+def IND(win, off):
+    return ("ind", win, off)
+
+
+def hits(x, y):
+    if x[0] >= y[1] or y[0] >= x[1]:
+        return False
+    return not (x[2] == y[2] and x[2] > 1 and (x[0] - y[0]) % x[2])
+
+
+def ordered(prog):
+    n = len(prog)
+    preds, succs = [set() for _ in range(n)], [set() for _ in range(n)]
+    acc = {}
+    for i, (e, ro, ri, c, f, lat, up) in enumerate(prog):
+        for lst, wr in ((ro, True), (ri, False)):
+            for (nm, a, b, s) in lst:
+                ps = nm in PSUMS
+                for (j, e2, a2, b2, s2, w2) in acc.get(nm, ()):
+                    if j != i and ((ps and e != e2) or ((wr or w2) and hits((a, b, s), (a2, b2, s2)))):
+                        preds[i].add(j)
+        for lst, wr in ((ro, True), (ri, False)):
+            for (nm, a, b, s) in lst:
+                old = acc.get(nm, [])
+                if wr and s == 1:
+                    old = [o for o in old if not (o[2] >= a and o[3] <= b and (nm not in PSUMS or o[1] == e))]
+                acc[nm] = old + [(i, e, a, b, s, wr)]
+    for i in range(n):
+        for j in preds[i]:
+            succs[j].add(i)
+    dur = [p[3] + (p[5] or 0.0) for p in prog]
+    tail = [0.0] * n
+    for i in range(n - 1, -1, -1):
+        tail[i] = prog[i][6] + dur[i] + max([tail[j] + WK for j in succs[i]] or [0.0])
+    left = [len(p) for p in preds]
+    ready = {i: 0.0 for i in range(n) if not left[i]}
+    free, out, when = {}, [], [0.0] * n
+    while ready:
+        t = min(max(r, free.get(prog[i][0], 0.0)) for i, r in ready.items())
+        best = None
+        for i, r in ready.items():
+            if max(r, free.get(prog[i][0], 0.0)) <= t + 0.02 and (best is None or (tail[i], -i) > (tail[best], -best)):
+                best = i
+        i = best
+        t = max(ready.pop(i), free.get(prog[i][0], 0.0))
+        if prog[i][0] != "a":
+            free[prog[i][0]] = t + prog[i][3]
+        out.append(i)
+        for j in succs[i]:
+            when[j] = max(when[j], t + dur[i] + WK)
+            left[j] -= 1
+            if not left[j]:
+                ready[j] = when[j]
+    return out
+
+
+def rank_program(g, core, T, topo):
+    rank = T.rank_of(core)
+    if rank is None:
+        return
+    N = len(T.cores)
+    queues = {"v": g.vector, "s": g.scalar, "t": g.tensor, "g": g, "y": g.sync}
+    semof = {"v": "sv", "s": "ss_", "t": "st", "g": "sg"}
+    tick = {"v": 0, "s": 0, "t": 0, "g": 0}
+    known = {e: {} for e in queues}
+    snaps = {}
+    acc = {}
+    prog = []
+    ndma, local, arrived = [0], [0], {}
+    first = [0.0]
+
+    def ap(v):
+        if v[0] == "ind":
+            return T[v[1][0]][:, v[1][1]:v[1][2]].indirect(T[v[2][0]][:, v[2][1]:v[2][2]])
+        n, a, b, s = v
+        return T[n][:, a:b] if s == 1 else T[n][:, a:b:s]
+
+    def need(e, outs, ins):
+        w = {}
+        for lst, wr in ((outs, True), (ins, False)):
+            for (n, a, b, s) in lst:
+                for (src, cnt, a2, b2, s2, wr2) in acc.get(n, []):
+                    if (src == e or n not in PSUMS) and (not (wr or wr2) or not hits((a, b, s), (a2, b2, s2))):
+                        continue
+                    w[src] = max(w.get(src, 0), cnt)
+        k = known[e]
+        w = {s: c for s, c in w.items() if k.get(s, 0) < c}
+        for s, c in list(w.items()):
+            if any(s2 != s and snaps[(s2, c2)].get(s, 0) >= c for s2, c2 in w.items()):
+                w.pop(s)
+        for s, c in w.items():
+            queues[e].wait_ge(T.sem[semof.get(s, s)], c)
+            for s2, c2 in [(s, c)] + list(snaps[(s, c)].items()):
+                k[s2] = max(k.get(s2, 0), c2)
+
+    def note(e, src, cnt, outs, ins):
+        snaps[(src, cnt)] = dict(known[e]) if e else {}
+        for lst, wr in ((outs, True), (ins, False)):
+            for (n, a, b, s) in lst:
+                old = acc.get(n, [])
+                if wr and s == 1:
+                    old = [o for o in old if not (o[2] >= a and o[3] <= b and (n not in PSUMS or o[0] == src))]
+                else:
+                    old = [o for o in old if not (o[0] == src and o[2:] == (a, b, s, wr))]
+                acc[n] = old + [(src, cnt, a, b, s, wr)]
+
+    def op(e, outs, ins, calls, cost):
+        ro = [v[1] if v[0] == "ind" else v for v in outs]
+        ri = [v[2] for v in outs if v[0] == "ind"]
+        for v in ins:
+            ri += [v[1], v[2]] if v[0] == "ind" else [v]
+
+        def emit():
+            need(e, ro, ri)
+            for c in calls[:-1]:
+                c()
+            tick[e] += 1
+            calls[-1]().then_inc(T.sem[semof[e]], 1)
+            note(e, e, tick[e], ro, ri)
+        prog.append((e, ro, ri, cost + 0.05, emit, None, first[0]))
+
+    def num(v):
+        return 16 * (v[2][2] - v[2][1]) if v[0] == "ind" else (v[2] - v[1] + v[3] - 1) // v[3]
+
+    def tm(n, *vs):
+        two = all(SCRATCH[v[0]][2] in ("bfloat16", "float16") for v in vs)
+        return CY * max(64, n * (0.5 if two else 1))
+
+    def vcopy(o, i):
+        n = num(i)
+        op("v", [o], [i], [lambda: g.vector.tensor_copy(ap(o), ap(i))],
+           3.8 * CY * n if o[0] == "ind" else 1.56 * CY * n if i[0] == "ind" else tm(n, o, i))
+
+    def vtt(o, a, b, f):
+        op("v", [o], [a, b], [lambda: g.vector.tensor_tensor(ap(o), ap(a), ap(b), f)],
+           CY * max(64, num(b) * (1 if a[0] in PSUMS or b[0] in PSUMS else 2)))
+
+    def vts(o, a, s1, f1, s2=None, f2=None):
+        x1 = ap(s1) if isinstance(s1, tuple) else s1
+        cols = [s1] if isinstance(s1, tuple) else []
+        if f2 is None:
+            op("v", [o], [a] + cols, [lambda: g.vector.tensor_scalar(ap(o), ap(a), x1, None, f1)], tm(num(a), o, a))
+        else:
+            op("v", [o], [a] + cols, [lambda: g.vector.tensor_scalar(ap(o), ap(a), x1, s2, f1, f2)], tm(num(a), o, a))
+
+    def vset(o, c):
+        op("v", [o], [], [lambda: g.vector.memset(ap(o), c)], tm(num(o)))
+
+    def sact(o, i, f=AF.Copy, bias=0.0, scale=1.0):
+        n = num(i)
+        col = isinstance(bias, tuple)
+        bb = ap(bias) if col else bias
+        op("s", [o], [i] + ([bias] if col else []), [lambda: g.scalar.activation(ap(o), ap(i), f, bias=bb, scale=scale)],
+           CY * (1.56 * n if i[0] == "ind" else max(64, n)))
+
+    def mm(o, terms, start=True, stop=True):
+        n = len(terms)
+        op("t", [o], [x for t in terms for x in t],
+           [lambda k=k: g.tensor.matmul(ap(o), ap(terms[k][0]), ap(terms[k][1]), start and k == 0, stop and k == n - 1)
+            for k in range(n)],
+           sum(max(64, num(t[1])) for t in terms) * CY * (4 if SCRATCH[terms[0][0][0]][2] == "float32" else 1))
+
+    def asel(o, i, pat, cmp, base, cm):
+        op("g", [o], [i], [lambda: g.affine_select(ap(o), ap(i), pat, cmp, 0.0, base, cm)], 0.17 + 2 * CY * num(o))
+
+    def iota(o, pat, base, cm):
+        if SCRATCH[o[0]][2] == "int32":
+            op("g", [o], [], [lambda: g.iota(ap(o), pat, base, cm)], 0.13 + 2 * CY * num(o))
+        else:
+            op("g", [o], [], [lambda: g.iota(ap(o), pat, base, cm, allow_small_or_imprecise_dtypes=True)],
+               0.13 + 2 * CY * num(o))
+
+    def dma(o_ap, i_ap, outs, ins):
+        def emit():
+            need("y", outs, ins)
+            s = "d%d" % ndma[0]
+            ndma[0] += 1
+            g.sync.dma_start(o_ap, i_ap).then_inc(T.sem[s], 16)
+            note("y", s, 16, outs, ins)
+        prog.append(("y", outs, ins, 0.1, emit, 2.5, first[0]))
+
+    peers = {d: T.cores[(rank + d) % N] for d in (1, 2, 3)}
+    homes = {d: T.cores[(rank - d) % N] for d in (1, 2, 3)}
+
+    def split(src, dsts):
+        away = [c for c in dsts if topo.chip(c) != topo.chip(src)]
+        pool = topo.engines(src, away[0])
+        n = len(pool) // len(away)
+        res = {c: pool[k * n:(k + 1) * n] for k, c in enumerate(away)}
+        for c in dsts:
+            if c not in res:
+                res[c] = [e for e in topo.engines(src, c) if e not in pool]
+        return res
+
+    def send(to, pieces, sems, ins, guard=()):
+        m = split(core, [to[d] for d in (1, 2, 3)])
+        tr = []
+        for d in (1, 2, 3):
+            rid, pid, _ = topo.addr(to[d])
+            n = len(m[to[d]]) // len(pieces)
+            for k, (sn, sc, dn, dc) in enumerate(pieces):
+                c = (d - 1) * B
+                tr.append(RemoteDMATransfer(
+                    dst_ids=[DstId(rid=rid, pnc=pid)], dma_engine_mask=sum(1 << e for e in m[to[d]][k * n:(k + 1) * n]),
+                    remote_sem=T.sem[sems + str(d)], src=T[sn][:, sc + c:sc + c + B], dst=T[dn][:, dc + c:dc + c + B]))
+                local[0] += n
+        guard = list(guard)
+
+        def emit():
+            need("g", guard, ins)
+            g.remote_dma_fused(tr, local_sem=T.sem["loc"])
+        prog.append(("g", guard + [("sent" + sems, 0, 1, 1)], ins, 1.0, emit, None, first[0]))
+
+    def recv(sems, frm, pieces):
+        for d in (1, 2, 3):
+            r = T.rank_of(frm[d])
+            s = 1 if frm is homes else -1
+            n = len(split(frm[d], [T.cores[(r + s * j) % N] for j in (1, 2, 3)])[core]) // len(pieces) * len(pieces)
+            c = (d - 1) * B
+            ro = [R(nm, cc + c, cc + c + B) for nm, cc in pieces]
+            arrived[sems + str(d)] = n
+            prog.append(("a", ro, [("sent" + sems, 0, 1, 1)], 0.0,
+                         lambda d=d, n=n, ro=ro: note(None, sems + str(d), n, ro, []), 5.0, 0.0))
+
+    rings = {"f": [0, NF], "q": [0, 2], "t": [0, NT]}
+    pools = {"a": [0, 1, 2], "c": [0, 1, 2, 4, 5, 6, 7], "z": [0, 1, 2, 3, 4, 5, 6, 7]}
+    pool, pr = ["c"], [0]
+
+    def ring(c):
+        rings[c][0] = (rings[c][0] + 1) % rings[c][1]
+        return "%s%d" % (c, rings[c][0])
+
+    def F(n=512):
+        return R(ring("f"), 0, n)
+
+    def PB():
+        pr[0] += 1
+        return "p%d" % pools[pool[0]][pr[0] % len(pools[pool[0]])]
+
+    def PQ(n=512):
+        return R(PB(), 0, n)
+
+    CH = [(512 * k, 512 * k + 512) for k in range(4)] + [(V, W)]
+    LSB = {d: R("ls", 8 * (d - 1), 8 * d) for d in (1, 2, 3)}
+    LSA = R("ls", 0, 24)
+    THR = R("th32", 0, 1)
+    XA, KEY = R("xa", 0, W), R("key", 0, W)
+
+    dma(T.x0i[:, 0:2048], T.x0[:], [R("x0i", 0, 2048)], [])
+    dma(T.x0i[:, 2352:2376], T.shw[:], [R("x0i", 2352, 2376)], [])
+    dma(T.x0i[:, 2048:2352], T.nxt[:], [R("x0i", 2048, 2352)], [])
+    dma(T.x0i[:, 2376:2377], T.th[:], [R("x0i", 2376, 2377)], [])
+    iota(R("pci", 0, 1), [[0, 1]], 0, 1)
+    iota(R("t0", 0, 512), [[64, 8], [0, 64]], 0, 0)
+    iota(R("t1", 0, 512), [[0, 8], [1, 64]], 0, 0)
+    vset(R("one", 0, 1024), 1.0)
+    vset(R("blk", 0, 128), 1.0)
+    vset(R("sel", 0, 128), 1.0)
+    vset(R("unh", 0, 2048), 0.0)
+    vset(R("unl", 0, 2048), 0.0)
+    asel(R("sel", 0, 128), R("sel", 0, 128), [[-16, 8], [0, 16]], OP.is_ge, 0, 1)
+    asel(R("sel", 0, 128), R("sel", 0, 128), [[16, 8], [0, 16]], OP.is_ge, 1, -1)
+    asel(R("blk", 0, 128), R("blk", 0, 128), [[-16, 8], [0, 16]], OP.is_ge, 0, 1)
+    asel(R("blk", 0, 128), R("blk", 0, 128), [[16, 8], [0, 16]], OP.is_ge, 15, -1)
+    asel(R("idn", 0, 128), R("one", 0, 128), [[-1, 128]], OP.is_equal, 0, 1)
+    vts(R("pci", 1, 2), R("pci", 0, 1), 1, OP.bitwise_and)
+    vts(R("pci", 2, 3), R("pci", 0, 1), 15, OP.bitwise_and)
+    vcopy(R("col", 0, 1), R("pci", 1, 2))
+    vts(R("col", 1, 2), R("col", 0, 1), -1.0, OP.mult, 1.0, OP.add)
+    vcopy(R("col", 2, 3), R("pci", 2, 3))
+    for b in range(1, 10):
+        vts(R("col", 2 + b, 3 + b), R("col", 1, 2), 512.0 * b, OP.mult)
+    vts(R("t2", 0, 512), R("t0", 0, 512), R("col", 1, 2), OP.mult)
+    vts(R("t3", 0, 512), R("t1", 0, 512), R("col", 0, 1), OP.mult)
+    vtt(R("phl", 0, 512), R("t2", 0, 512), R("t3", 0, 512), OP.add)
+    first[0] = 100.0
+    vcopy(R("ls", 0, 24), R("x0i", 2352, 2376))
+    for k in range(2):
+        vcopy(R("xa", 1024 * k, 1024 * k + 1024), R("x0i", 1024 * k, 1024 * k + 1024))
+    sact(R("sx", 0, GH), IND(R("xa", 0, V), LSA))
+    send(peers, [("sx", 0, "xa", V)], "ax1_", [R("sx", 0, GH)])
+    recv("ax1_", homes, [("xa", V)])
+    first[0] = 0.0
+    vcopy(R("lpn", 0, 304), R("x0i", 2048, 2352))
+    for b in range(1, 10):
+        n = min(512, P2 - 512 * b)
+        sact(R("phl", 512 * b, 512 * b + n), R("phl", 0, n), AF.Identity, bias=R("col", 2 + b, 3 + b))
+    vts(R("x0i", 0, 304), R("x0i", 2048, 2352), 1, OP.arith_shift_right)
+    vcopy(R("l1n", 0, 304), R("x0i", 0, 304))
+    vcopy(IND(R("pvh", 0, P2), R("lpn", 0, 256)), R("phl", 0, 4096))
+    vcopy(IND(R("pvh", 0, P2), R("lpn", 256, 304)), R("phl", 4096, P2))
+    vset(R("wrp", 0, 2048), 0.0)
+    vset(R("rdp", 0, 1024), 0.0)
+    vset(R("rdn", 0, 1024), 0.0)
+    vset(R("swp", 0, 128), 1.0)
+    vset(R("qr", 0, 128), 3.0 / 1024.0)
+    vset(R("nm", 0, V), 0.0)
+    for d in (1, 2, 3):
+        vcopy(IND(R("nm", 0, V), LSB[d]), R("one", 0, 128))
+    vcopy(THR, R("x0i", 2376, 2377))
+    sact(R("neg", 0, 128), R("idn", 0, 128), scale=-1.0)
+    sact(R("ngq", 0, 128), R("idn", 0, 128), scale=-0.25)
+    sact(R("d25", 0, 128), R("idn", 0, 128), scale=33554432.0)
+    sact(R("blp", 0, 128), R("blk", 0, 128), scale=4096.0)
+    sact(R("bln", 0, 128), R("blk", 0, 128), scale=-4096.0)
+    sact(R("ghl", 0, 768), R("phl", 4096, P2))
+    for k in range(16):
+        sact(R("wrp", 129 * k, 128 * k + 128, 16), R("sel", k, 128, 16))
+    asel(R("unh", 0, 2048, 2), R("one", 0, 1024), [[-1, 16], [-16, 8], [0, 8]], OP.is_equal, 0, 1)
+    asel(R("unl", 1, 2048, 2), R("one", 0, 1024), [[-1, 16], [-16, 8], [0, 8]], OP.is_equal, 0, 1)
+    asel(R("swp", 0, 128, 2), R("swp", 0, 128, 2), [[-2, 64]], OP.is_equal, -1, 1)
+    asel(R("swp", 1, 128, 2), R("swp", 1, 128, 2), [[-2, 64]], OP.is_equal, 0, 1)
+    iota(R("pid", 0, 304), [[16, 304]], 0, 0)
+    vts(R("pid", 0, 304), R("pid", 0, 304), R("col", 2, 3), OP.add)
+    vcopy(R("nxf", 0, 304), R("x0i", 2048, 2352))
+    vcopy(R("idh", 0, 128), R("idn", 0, 128))
+    vcopy(R("neh", 0, 128), R("neg", 0, 128))
+    vcopy(R("nqh", 0, 128), R("ngq", 0, 128))
+
+    def wrap(flat, wf, lp, ln):
+        pb = PQ(304)
+        mm(pb, [(R("wrp", 128 * i, 128 * i + 128), R(flat, i, P2, 16)) for i in range(16)])
+        vcopy(R("x0i", 304, 608), pb)
+        sact(R(wf, 0, 304), pb)
+        vts(R("x0i", 608, 912), R("x0i", 304, 608), 1, OP.arith_shift_right)
+        vcopy(R(ln, 0, 304), R("x0i", 608, 912))
+        vcopy(R(lp, 0, 304), R("x0i", 304, 608))
+
+    def partners(wf, dn, dp):
+        pb = PQ(256)
+        mm(pb, [(R("swp", 0, 128), R(wf, 0, 256))])
+        vtt(R(dn, 0, 256), pb, R(wf, 0, 256), OP.subtract)
+        vtt(R(dp, 0, 256), R(wf, 0, 256), R("pid", 0, 256), OP.subtract)
+
+    def lst(l, c, k):
+        return R("l%d%s" % (l, c), CH[k][0] // 8, CH[k][1] // 8)
+
+    def gath(eng, o, win, off):
+        (sact if eng == "s" else vcopy)(o, IND(win, off))
+
+    def pairs(l, k, win, f, out, bias=0.0):
+        n = 2 * (CH[k][1] - CH[k][0])
+        qn = ring("q")
+        q = R(qn, 0, n)
+        sact(q, IND(win, lst(l, "n", k)), AF.Identity if bias else AF.Copy, bias=bias)
+        vtt(q, IND(win, lst(l, "p", k)), q, f)
+        vtt(out, R(qn, 0, n, 2), R(qn, 1, n, 2), f)
+
+    for k in range(5):
+        a, b = CH[k]
+        gath("s", R("fnx", 2 * a, 2 * b), XA, lst(1, "n", k))
+    for i in range(8):
+        for h in (0, 1):
+            m = 2 * i + h
+            sact(R("rdp", 128 * i + m, 128 * i + 128, 16), R("blk", m, 128, 16))
+            sact(R("rdn", 128 * i + m, 128 * i + 128, 16), R("blk", m, 128, 16), scale=-1.0)
+    wrap("pvh", "pvf", "lpp", "l1p")
+    partners("nxf", "dnn", "dpn")
+    partners("pvf", "dnp", "dpp")
+
+    for l in (1, 2, 3):
+        LVn = "lv%d" % l
+        srcs = {1: [("fpv", "fnx")], 2: [("ga", "gb")], 3: [("fpv", "fnx"), ("pvh", "nxh")]}[l]
+        I1, NI, NQ = [R(x, 0, 128) for x in (("idh", "neh", "nqh") if l == 2 else ("idn", "neg", "ngq"))]
+        pool[0] = "a"
+        zb = {}
+
+        def gathers(k):
+            a, b = CH[k]
+            o = -2 * a if l == 2 and k == 4 else 0
+            a2, b2 = o + 2 * a, o + 2 * b
+            fp, fn = srcs[0]
+            if l == 1:
+                gath("v" if k % 2 == 0 else "s", R(fp, a2, b2), XA, lst(1, "p", k))
+            else:
+                gath("v", R(fn, a2, b2), XA, lst(l, "n", k))
+                gath("v", R(fp, a2, b2), XA, lst(l, "p", k))
+            if l == 3:
+                for s, c in (("nxh", "n"), ("pvh", "p")):
+                    sact(R(s, a2, b2), IND(R("phl", W, P2), lst(l, c, k)), AF.Identity, bias=-0.375)
+            zb[k] = R("p%d" % (4 + k), 0, 512) if k < 4 else PQ(b - a)
+            mm(zb[k], [(NQ, R(p[1], a2 + h, b2, 2)) for p in srcs for h in (0, 1)] +
+               ([(R("qr", 0, 128), R("one", 0, b - a))] if l < 3 else []), stop=False)
+            mm(zb[k], [(NQ, R(p[0], a2 + h, b2, 2)) for p in srcs for h in (0, 1)], start=False)
+
+        def detail(k):
+            a, b = CH[k]
+            n = b - a
+            xm = F(n)
+            sact(xm, R("xa", a, b), AF.Identity, bias=-MG)
+            sact(zb[k], zb[k], AF.Identity, bias=MG)
+            d, e = (R("dd", a, b), R("ad", a, b)) if k < 4 else (F(n), F(n))
+            vtt(d, zb[k], xm, OP.add)
+            sact(e, d, AF.Abs)
+            t = R(ring("t"), 0, n)
+            if l == 1:
+                sact(t, e)
+            else:
+                sact(t, e, AF.Relu, bias=255.0, scale=-1.0)
+            terms = [(R("sel", 0, 128), R("phl", a, b)), (R("blp" if l == 1 else "bln", 0, 128), t)]
+            mm(zb[k], terms)
+            sact(R("key", a, b), zb[k])
+            if k < 4:
+                mm(zb[k], [(R("d25", 0, 128), R(x, a, b)) for x in ["nm"] + ["lv%d" % j for j in range(1, l)]] + terms)
+
+        def pack(k):
+            a, b = CH[k]
+            d, e = R("dd", a, b), R("ad", a, b)
+            q, w = F(), F()
+            m, ds = PQ(), PQ()
+            sact(q, d, AF.Identity, bias=-0.375, scale=0.25)
+            sact(q, q, AF.Identity, bias=MG)
+            sact(ds, q, AF.Identity, bias=-MG)
+            vts(m, e, THR, OP.is_ge)
+            if l < 3:
+                sact(w, m, AF.Identity, bias=KP)
+            else:
+                sact(w, m, AF.Identity, bias=1.0, scale=-1.0)
+            vtt(d, m, d, OP.mult)
+            vtt(e, ds, w, OP.mult)
+
+        def chosen(k):
+            a, b = CH[k]
+            f = F()
+            pairs(l, k, KEY, OP.min, f)
+            vtt(R(LVn, a, b), zb[k], f, OP.is_lt)
+
+        def likeness(k):
+            a, b = CH[k]
+            terms = []
+            for x, y, sg in ((0, 0, "rdp"), (1, 1, "rdp"), (0, 1, "rdn"), (1, 0, "rdn")):
+                u = PQ()
+                mm(u, [(I1, R(s[0], 2 * a + x, 2 * b, 2)) for s in srcs] + [(NI, R(s[1], 2 * a + y, 2 * b, 2)) for s in srcs])
+                tn = ring("t")
+                sact(R(tn, 0, 512), u, AF.Abs)
+                if l > 1:
+                    vts(R(tn, 0, 512), R(tn, 0, 512), 255.0, OP.min)
+                terms += [(R(sg, 128 * i, 128 * i + 128), R(tn, i, 512, 8)) for i in range(8)]
+            mm(R("p3", 64 * k, 64 * k + 64), terms)
+
+        def links_small():
+            lb = PB()
+            for k in range(4):
+                a, b = CH[k]
+                mm(R(lb, 64 * k, 64 * k + 64), [(R("rdp", 128 * i, 128 * i + 128), R(LVn, a + i, b, 8)) for i in range(8)])
+            sact(R("lw", 0, 256), R(lb, 0, 256), scale=1.0 / 16)
+            vts(R("lc", 0, 256), R("p3", 0, 256), 0.0, OP.is_gt)
+            vtt(R("lc", 0, 256), R("lc", 0, 256), R("lw", 0, 256), OP.mult)
+            for (dn, dp, h, lo) in (("dnn", "dpn", "hn", "ln_"), ("dnp", "dpp", "hp", "lp_"))[:2 if l < 3 else 1]:
+                vtt(R("w0", 0, 256), R("lc", 0, 256), R(dn, 0, 256), OP.mult)
+                vtt(R("w1", 0, 256), R("lw", 0, 256), R(dp, 0, 256), OP.mult)
+                vtt(R("w0", 0, 256), R("w0", 0, 256), R("w1", 0, 256), OP.add)
+                vtt(R("w0", 0, 256), R("w0", 0, 256), R("pid", 0, 256), OP.add)
+                sact(R(h, 0, 256), R("w0", 0, 256))
+                vtt(R(lo, 0, 256), R("w0", 0, 256), R(h, 0, 256), OP.subtract)
+
+        def unwrap(fn, h, lo):
+            if l != 2:
+                sact(R(fn, 4096, P2), R("ghl", 0, 768))
+            for i in range(16):
+                if i % 2 == 0:
+                    bn = PB()
+                bk = R(bn, 256 * (i % 2), 256 * (i % 2) + 256)
+                mm(bk, [(R("unh", 128 * i, 128 * i + 128), R(h, 0, 256)), (R("unl", 128 * i, 128 * i + 128), R(lo, 0, 256))])
+                sact(R(fn, i, 4096, 16), bk)
+
+        def own(k):
+            a, b = CH[k]
+            x, b1, b2 = R("xa", a, b), PQ(), PQ()
+            if l < 3:
+                s = R("sp%d" % l, a, b)
+                pairs(l, k, KEY, OP.add, s)
+                z = F()
+                sact(z, s, AF.Identity, bias=MG * KP)
+                sact(b1, z, AF.Identity, bias=-MG, scale=1.0 / KP)
+                sact(b2, z, AF.Identity, bias=-MG * KP)
+                vtt(x, b1, x, OP.add)
+                vtt(s, s, b2, OP.subtract)
+            else:
+                sact(b2, R(LVn, a, b), scale=-BIG)
+                vtt(x, b2, x, OP.add)
+                pairs(l, k, KEY, OP.add, b1)
+                vtt(x, b1, x, OP.add)
+
+        def border(buf, rc):
+            for d in (1, 2, 3):
+                c = rc + (d - 1) * B
+                vtt(R("bt", 0, 128), IND(R(buf, 0, V), LSB[d]), R(rs, c, c + B), OP.add)
+                vcopy(IND(R(buf, 0, V), LSB[d]), R("bt", 0, 128))
+
+        def kept(k):
+            a, b = CH[k]
+            f, b1, b2 = F(), PQ(), PQ()
+            sact(b2, R("dd", a, b), AF.Identity, bias=BIG)
+            vtt(f, b2, R(LVn, a, b), OP.mult)
+            sact(R("dd" if l == 3 else "dl%d" % l, a, b), f, AF.Identity, bias=-BIG if l == 1 else -(BIG + MG))
+            if l < 3:
+                s = R("sp%d" % l, a, b)
+                sact(b1, R(LVn, a, b), scale=BIG)
+                vtt(s, b1, s, OP.add)
+
+        if l == 3:
+            for k in range(5):
+                a, b = CH[k]
+                t = R(ring("t"), 0, b - a)
+                sact(t, R("xa", a, b))
+                vtt(R("phl", W + a, W + b), R("xa", a, b), t, OP.subtract)
+        order = [4, 0, 1, 2, 3] if l > 1 else [0, 1, 2, 3, 4]
+        for i in range(6):
+            if i < 5:
+                gathers(order[i])
+            if i > 0:
+                detail(order[i - 1])
+        for k in (0, 1):
+            pack(k)
+        for k in range(4):
+            chosen(k)
+            if k < 2:
+                pack(k + 2)
+            if k < (4 if l < 3 else 2):
+                likeness(k)
+        pool[0] = "c"
+        vset(R("key", V, W), 0.0)
+        for k in range(4):
+            a, b = CH[k]
+            vtt(R("key", a, b), R("ad", a, b), R(LVn, a, b), OP.mult)
+        rs = "rs2" if l == 2 else "rs1"
+        xg = [R("xa", V, W)]
+        if l < 3:
+            q, z, b4 = F(GH), F(GH), PQ(GH)
+            pairs(l, 4, KEY, OP.add, q)
+            sact(z, q, AF.Identity, bias=MG * KP)
+            sact(b4, z, AF.Identity, bias=-MG * KP)
+            sact(R("ss", 0, GH), z, AF.Identity, bias=-MG, scale=1.0 / KP)
+            vtt(R("ss", GH, 768), q, b4, OP.subtract)
+            send(homes, [("ss", 0, rs, 0), ("ss", GH, rs, GH)], "as%d_" % l, [R("ss", 0, 768)], xg)
+            recv("as%d_" % l, peers, [(rs, 0), (rs, GH)])
+            links_small()
+            own(0)
+            own(1)
+            unwrap("fnx", "hn", "ln_")
+            own(2)
+            own(3)
+            border("xa", 0)
+            sact(R("sx", 0, GH), IND(R("xa", 0, V), LSA))
+            send(peers, [("sx", 0, "xa", V)], "ax%d_" % (l + 1), [R("sx", 0, GH)], [R("rs1", 0, 768)] if l == 2 else [])
+            recv("ax%d_" % (l + 1), homes, [("xa", V)])
+            unwrap("fpv", "hp", "lp_")
+            gath("v", R("nxh", 0, 4096), R("fnx", 0, P2), R("lpn", 0, 256))
+            gath("s", R("nxh", 4096, P2), R("fnx", 0, P2), R("lpn", 256, 304))
+            gath("s", R("pvh", 0, 3584), R("fpv", 0, P2), R("lpp", 0, 224))
+            gath("v", R("pvh", 3584, P2), R("fpv", 0, P2), R("lpp", 224, 304))
+            wrap("nxh", "nxf", "lpn", "l%dn" % (l + 1))
+            border("sp%d" % l, GH)
+            sact(R("sg%d" % l, 0, GH), IND(R("sp%d" % l, 0, V), LSA))
+            for k in range(4):
+                kept(k)
+            wrap("pvh", "pvf", "lpp", "l%dp" % (l + 1))
+            partners("nxf", "dnn", "dpn")
+            if l < 2:
+                partners("pvf", "dnp", "dpp")
+        else:
+            pairs(l, 4, KEY, OP.add, R("ss", 0, GH))
+            send(homes, [("ss", 0, rs, 0)], "as3_", [R("ss", 0, GH)], xg)
+            recv("as3_", peers, [(rs, 0)])
+            for k in range(4):
+                own(k)
+            border("xa", 0)
+            sact(R("bs", 0, GH), IND(R("xa", 0, V), LSA))
+            vtt(R("bs", GH, 2 * GH), R("bs", 0, GH), R("sg2", 0, GH), OP.subtract)
+            vtt(R("bs", 2 * GH, 3 * GH), R("bs", GH, 2 * GH), R("sg1", 0, GH), OP.subtract)
+            send(peers, [("bs", 0, "xa", V)], "ab3_", [R("bs", 0, GH)])
+            send(peers, [("bs", GH, "rb2", 0), ("bs", 2 * GH, "rb1", 0)], "ab2_", [R("bs", GH, 3 * GH)])
+            recv("ab3_", homes, [("xa", V)])
+            recv("ab2_", homes, [("rb2", 0), ("rb1", 0)])
+            for k in range(4):
+                kept(k)
+            sact(R("key", V, W), R("rb2", 0, GH))
+            likeness(2)
+            likeness(3)
+            links_small()
+            unwrap("fnx", "hn", "ln_")
+
+    pool[0] = "z"
+
+    def undo(l, src, dst, dl, sp):
+        fms = {}
+        for k in range(5):
+            if k < 4:
+                z, fms[k] = PQ(), PQ()
+                pairs(l, k, R(src, 0, W), OP.add, z, -0.75)
+                sact(fms[k], z, AF.Identity, bias=MG, scale=0.25)
+            if k > 0:
+                a, b = CH[k - 1]
+                y, mx = PQ(), PQ()
+                vtt(y, fms[k - 1], R(dl, a, b), OP.add)
+                if sp is None:
+                    vtt(R(dst, a, b), y, R(src, a, b), OP.max)
+                    dma(T.yx[:, a:b], T[dst][:, a:b], [], [R(dst, a, b)])
+                else:
+                    vtt(mx, y, R(src, a, b), OP.max)
+                    vtt(R(dst, a, b), mx, R(sp, a, b), OP.subtract)
+
+    undo(3, "xa", "key", "dd", "sp2")
+    for k in range(4):
+        a, b = CH[k]
+        sact(R("sp2", a, b), R("dl1", a, b), AF.Identity, bias=-MG)
+    sact(R("xa", V, W), R("rb1", 0, GH))
+    gath("v", R("nxh", 0, 2432), R("fnx", 0, P2), R("lpn", 0, 152))
+    gath("s", R("nxh", 2432, P2), R("fnx", 0, P2), R("lpn", 152, 304))
+    undo(2, "key", "xa", "dl2", "sp1")
+    for k in range(10):
+        a, b = 512 * k, min(512 * k + 512, P2)
+        bk = PQ(b - a)
+        mm(bk, [(R("sel", 0, 128), R("nxh", a, b))])
+        o = R("dd", a, b) if k < 4 else R("ad", a - V, b - V) if k < 8 else R("f%d" % (k - 8), 0, b - a)
+        sact(o, bk)
+        if k == 3 or k == 7:
+            nm = "dd" if k == 3 else "ad"
+            dma(T.yn[:, b - V:b], T[nm][0:128:16, 0:V], [], [R(nm, 0, V)])
+        if k >= 8:
+            dma(T.yn[:, a:b], T[o[0]][0:128:16, 0:b - a], [], [o])
+    undo(1, "xa", "key", "sp2", None)
+
+    for i in ordered(prog):
+        prog[i][4]()
+
+    for e in ("v", "s", "t", "g"):
+        g.wait_ge(T.sem[semof[e]], tick[e])
+    for k in range(ndma[0]):
+        g.wait_ge(T.sem["d%d" % k], 16)
+    for s, n in arrived.items():
+        g.wait_ge(T.sem[s], n)
+    g.wait_ge(T.sem["loc"], local[0])

@@ -7,35 +7,36 @@ MG = 12582912.0
 KP = 4096.0
 BIG = 1048576.0
 
+TU = {"CY": 0.0009, "PCY": 0.0006, "WK": 0.1, "OV": 0.05, "GA": 1.4, "TT": 1.8, "VPEN": 0.6}
 SCRATCH = {}
 for _n, _c, _t in (
-        ("xa", W, "float32"), ("key", W, "float32"), ("dd", V, "float32"), ("ad", V, "float32"),
-        ("sp1", V, "float32"), ("sp2", V, "float32"), ("dl1", V, "bfloat16"), ("dl2", V, "float32"),
-        ("ga", 4096, "float16"), ("gb", 4096, "float16"), ("fnx", P2, "bfloat16"), ("fpv", P2, "bfloat16"),
+        ("xa", W, "float32"), ("key", W, "float32"), ("dd", V, "float32"),
+        ("sp1", V, "float32"), ("sp2", V, "float32"), ("dl1", V, "float32"), ("dl2", V, "float32"),
+        ("ga", P2, "float16"), ("gb", P2, "float16"), ("fnx", P2, "bfloat16"), ("fpv", P2, "bfloat16"),
         ("nxh", P2, "bfloat16"), ("pvh", P2, "bfloat16"), ("phl", P2, "bfloat16"), ("ghl", 768, "bfloat16"),
         ("lv1", V, "bfloat16"), ("lv2", V, "bfloat16"), ("lv3", V, "bfloat16"), ("nm", V, "bfloat16"),
-        ("q0", 1024, "float32"), ("q1", 1024, "float32"),
-        ("unh", 2048, "bfloat16"), ("unl", 2048, "bfloat16"), ("wrp", 2048, "bfloat16"),
-        ("rdp", 1024, "bfloat16"), ("rdn", 1024, "bfloat16"),
+        ("tk", V, "bfloat16"), ("un", 2052, "bfloat16"), ("wz", 144, "bfloat16"), ("wq", 144, "bfloat16"),
+        ("rz", 144, "bfloat16"), ("rn", 144, "bfloat16"),
         ("idn", 128, "bfloat16"), ("neg", 128, "bfloat16"), ("ngq", 128, "bfloat16"), ("d25", 128, "bfloat16"),
         ("blk", 128, "bfloat16"), ("blp", 128, "bfloat16"), ("bln", 128, "bfloat16"), ("sel", 128, "bfloat16"),
-        ("idh", 128, "float16"), ("neh", 128, "float16"), ("nqh", 128, "float16"), ("qr", 128, "bfloat16"),
-        ("swp", 128, "float32"), ("one", 1024, "bfloat16"),
+        ("seq", 128, "bfloat16"), ("mgc", 128, "bfloat16"),
+        ("idh", 128, "float16"), ("neh", 128, "float16"), ("nqh", 128, "float16"),
+        ("qr", 128, "bfloat16"), ("swp", 128, "float32"), ("one", 512, "bfloat16"), ("hlf", 128, "float32"),
+        ("pm00", 128, "float32"), ("pm01", 128, "float32"), ("pm10", 128, "float32"), ("pm11", 128, "float32"),
         ("x0i", 2380, "int32"), ("pci", 8, "int32"), ("col", 16, "float32"), ("th32", 8, "float32"), ("ls", 24, "uint16"),
-        ("pid", 304, "float32"), ("nxf", 304, "float32"), ("pvf", 304, "float32"),
+        ("pid", 304, "float32"), ("pih", 256, "float32"), ("nxf", 304, "float32"), ("pvf", 304, "float32"),
         ("dnn", 256, "float32"), ("dnp", 256, "float32"), ("dpn", 256, "float32"), ("dpp", 256, "float32"),
         ("lw", 256, "float32"), ("lc", 256, "float32"), ("w0", 256, "float32"), ("w1", 256, "float32"),
         ("hn", 256, "bfloat16"), ("hp", 256, "bfloat16"), ("ln_", 256, "bfloat16"), ("lp_", 256, "bfloat16"),
         ("lpn", 304, "uint16"), ("lpp", 304, "uint16"),
-        ("sx", GH, "float32"), ("ss", 768, "float32"), ("rs1", 768, "float32"), ("rs2", 768, "float32"),
+        ("ss", 768, "float32"), ("rs1", 768, "float32"), ("rs2", 768, "float32"),
         ("bs", 3 * GH, "float32"), ("rb1", GH, "float32"), ("rb2", GH, "float32"),
         ("sg1", GH, "float32"), ("sg2", GH, "float32"), ("bt", 128, "float32")):
     SCRATCH[_n] = ("sbuf", [128, _c], _t)
-NF, NT = 4, 6
-for _k in range(NF):
-    SCRATCH["f%d" % _k] = ("sbuf", [128, 512], "float32")
-for _k in range(NT):
-    SCRATCH["t%d" % _k] = ("sbuf", [128, 512], "bfloat16")
+RINGS = {"f": (6, "float32"), "q": (4, "float32"), "t": (6, "bfloat16"), "m": (2, "bfloat16")}
+for _r in RINGS:
+    for _k in range(RINGS[_r][0]):
+        SCRATCH["%s%d" % (_r, _k)] = ("sbuf", [128, 512], RINGS[_r][1])
 for _k in range(8):
     SCRATCH["p%d" % _k] = ("psum", [128, 512], "float32")
 for _k in (1, 2, 3):
@@ -44,8 +45,6 @@ for _k in (1, 2, 3):
 ARR = [a + str(d) for a in ("ax1_", "ax2_", "ax3_", "as1_", "as2_", "as3_", "ab3_", "ab2_") for d in (1, 2, 3)]
 SEMAPHORES = ["sv", "ss_", "st", "sg", "loc"] + ARR + ["d%d" % k for k in range(20)]
 PSUMS = ["p%d" % k for k in range(8)]
-CY = 0.00104
-WK = 0.1
 
 
 def R(name, a, b, s=1):
@@ -63,45 +62,52 @@ def hits(x, y):
 
 
 def ordered(prog):
-    n = len(prog)
+    n, WK = len(prog), TU["WK"]
     preds, succs = [set() for _ in range(n)], [set() for _ in range(n)]
     acc = {}
-    for i, (e, ro, ri, c, f, lat, up) in enumerate(prog):
+    for i, (var, ro, ri, lat, up) in enumerate(prog):
+        e = var[0][0] if len(var) == 1 else None
         for lst, wr in ((ro, True), (ri, False)):
             for (nm, a, b, s) in lst:
                 ps = nm in PSUMS
                 for (j, e2, a2, b2, s2, w2) in acc.get(nm, ()):
-                    if j != i and ((ps and e != e2) or ((wr or w2) and hits((a, b, s), (a2, b2, s2)))):
+                    if j != i and ((ps and (e is None or e != e2)) or ((wr or w2) and hits((a, b, s), (a2, b2, s2)))):
                         preds[i].add(j)
         for lst, wr in ((ro, True), (ri, False)):
             for (nm, a, b, s) in lst:
                 old = acc.get(nm, [])
                 if wr and s == 1:
-                    old = [o for o in old if not (o[2] >= a and o[3] <= b and (nm not in PSUMS or o[1] == e))]
+                    old = [o for o in old if not (o[2] >= a and o[3] <= b and
+                                                  (nm not in PSUMS or (e is not None and o[1] == e)))]
                 acc[nm] = old + [(i, e, a, b, s, wr)]
     for i in range(n):
         for j in preds[i]:
             succs[j].add(i)
-    dur = [p[3] + (p[5] or 0.0) for p in prog]
+    dur = [min(v[1] for v in p[0]) + (p[3] or 0.0) for p in prog]
     tail = [0.0] * n
     for i in range(n - 1, -1, -1):
-        tail[i] = prog[i][6] + dur[i] + max([tail[j] + WK for j in succs[i]] or [0.0])
+        tail[i] = prog[i][4] + dur[i] + max([tail[j] + WK for j in succs[i]] or [0.0])
     left = [len(p) for p in preds]
     ready = {i: 0.0 for i in range(n) if not left[i]}
     free, out, when = {}, [], [0.0] * n
+
+    def start(i, r):
+        return min(max(r, free.get(v[0], 0.0)) for v in prog[i][0])
     while ready:
-        t = min(max(r, free.get(prog[i][0], 0.0)) for i, r in ready.items())
+        t = min(start(i, r) for i, r in ready.items())
         best = None
         for i, r in ready.items():
-            if max(r, free.get(prog[i][0], 0.0)) <= t + 0.02 and (best is None or (tail[i], -i) > (tail[best], -best)):
+            if start(i, r) <= t + 0.02 and (best is None or (tail[i], -i) > (tail[best], -best)):
                 best = i
         i = best
-        t = max(ready.pop(i), free.get(prog[i][0], 0.0))
-        if prog[i][0] != "a":
-            free[prog[i][0]] = t + prog[i][3]
-        out.append(i)
+        r = ready.pop(i)
+        var = min(prog[i][0], key=lambda v: max(r, free.get(v[0], 0.0)) + v[1] + (TU["VPEN"] if v[0] == "v" else 0.0))
+        t = max(r, free.get(var[0], 0.0))
+        if var[0] != "a":
+            free[var[0]] = t + var[1]
+        out.append(var[2])
         for j in succs[i]:
-            when[j] = max(when[j], t + dur[i] + WK)
+            when[j] = max(when[j], t + var[1] + (prog[i][3] or 0.0) + WK)
             left[j] -= 1
             if not left[j]:
                 ready[j] = when[j]
@@ -113,6 +119,7 @@ def rank_program(g, core, T, topo):
     if rank is None:
         return
     N = len(T.cores)
+    CY, PCY, GA = TU["CY"], TU["PCY"], TU["GA"]
     queues = {"v": g.vector, "s": g.scalar, "t": g.tensor, "g": g, "y": g.sync}
     semof = {"v": "sv", "s": "ss_", "t": "st", "g": "sg"}
     tick = {"v": 0, "s": 0, "t": 0, "g": 0}
@@ -158,20 +165,22 @@ def rank_program(g, core, T, topo):
                     old = [o for o in old if not (o[0] == src and o[2:] == (a, b, s, wr))]
                 acc[n] = old + [(src, cnt, a, b, s, wr)]
 
-    def op(e, outs, ins, calls, cost):
+    def op(outs, ins, *variants):
         ro = [v[1] if v[0] == "ind" else v for v in outs]
         ri = [v[2] for v in outs if v[0] == "ind"]
         for v in ins:
             ri += [v[1], v[2]] if v[0] == "ind" else [v]
 
-        def emit():
-            need(e, ro, ri)
-            for c in calls[:-1]:
-                c()
-            tick[e] += 1
-            calls[-1]().then_inc(T.sem[semof[e]], 1)
-            note(e, e, tick[e], ro, ri)
-        prog.append((e, ro, ri, cost + 0.05, emit, None, first[0]))
+        def emitter(e, calls):
+            def emit():
+                need(e, ro, ri)
+                for c in calls[:-1]:
+                    c()
+                tick[e] += 1
+                calls[-1]().then_inc(T.sem[semof[e]], 1)
+                note(e, e, tick[e], ro, ri)
+            return emit
+        prog.append(([(e, cost + TU["OV"], emitter(e, calls)) for e, calls, cost in variants], ro, ri, None, first[0]))
 
     def num(v):
         return 16 * (v[2][2] - v[2][1]) if v[0] == "ind" else (v[2] - v[1] + v[3] - 1) // v[3]
@@ -182,47 +191,64 @@ def rank_program(g, core, T, topo):
 
     def vcopy(o, i):
         n = num(i)
-        op("v", [o], [i], [lambda: g.vector.tensor_copy(ap(o), ap(i))],
-           3.8 * CY * n if o[0] == "ind" else 1.56 * CY * n if i[0] == "ind" else tm(n, o, i))
+        op([o], [i], ("v", [lambda: g.vector.tensor_copy(ap(o), ap(i))],
+                      3.8 * CY * n if o[0] == "ind" else GA * CY * n if i[0] == "ind" else tm(n, o, i)))
 
     def vtt(o, a, b, f):
-        op("v", [o], [a, b], [lambda: g.vector.tensor_tensor(ap(o), ap(a), ap(b), f)],
-           CY * max(64, num(b) * (1 if a[0] in PSUMS or b[0] in PSUMS else 2)))
+        op([o], [a, b], ("v", [lambda: g.vector.tensor_tensor(ap(o), ap(a), ap(b), f)],
+                         CY * max(64, num(b) * (1 if a[0] in PSUMS or b[0] in PSUMS else TU["TT"] if a[0] == "ind" else 2))))
 
     def vts(o, a, s1, f1, s2=None, f2=None):
         x1 = ap(s1) if isinstance(s1, tuple) else s1
         cols = [s1] if isinstance(s1, tuple) else []
         if f2 is None:
-            op("v", [o], [a] + cols, [lambda: g.vector.tensor_scalar(ap(o), ap(a), x1, None, f1)], tm(num(a), o, a))
+            op([o], [a] + cols, ("v", [lambda: g.vector.tensor_scalar(ap(o), ap(a), x1, None, f1)], tm(num(a), o, a)))
         else:
-            op("v", [o], [a] + cols, [lambda: g.vector.tensor_scalar(ap(o), ap(a), x1, s2, f1, f2)], tm(num(a), o, a))
+            op([o], [a] + cols, ("v", [lambda: g.vector.tensor_scalar(ap(o), ap(a), x1, s2, f1, f2)], tm(num(a), o, a)))
 
     def vset(o, c):
-        op("v", [o], [], [lambda: g.vector.memset(ap(o), c)], tm(num(o)))
+        op([o], [], ("v", [lambda: g.vector.memset(ap(o), c)], tm(num(o))))
 
     def sact(o, i, f=AF.Copy, bias=0.0, scale=1.0):
         n = num(i)
         col = isinstance(bias, tuple)
         bb = ap(bias) if col else bias
-        op("s", [o], [i] + ([bias] if col else []), [lambda: g.scalar.activation(ap(o), ap(i), f, bias=bb, scale=scale)],
-           CY * (1.56 * n if i[0] == "ind" else max(64, n)))
+        op([o], [i] + ([bias] if col else []),
+           ("s", [lambda: g.scalar.activation(ap(o), ap(i), f, bias=bb, scale=scale)],
+            CY * (GA * n if i[0] == "ind" else max(64, n)) + 0.01))
+
+    def lin(o, i, scale=1.0, bias=0.0, relu=False):
+        n = num(i)
+        ind = i[0] == "ind"
+        sv = ("s", [lambda: g.scalar.activation(ap(o), ap(i), AF.Relu if relu else AF.Identity, bias=bias, scale=scale)],
+              CY * (GA * n if ind else max(64, n)) + 0.01)
+        tv = CY * GA * n if ind else tm(n, o, i)
+        if relu:
+            vv = ("v", [lambda: g.vector.tensor_scalar(ap(o), ap(i), 0.0, None, OP.max)], tv)
+        elif scale == 1.0 and bias == 0.0:
+            vv = ("v", [lambda: g.vector.tensor_copy(ap(o), ap(i))], tv)
+        elif scale == 1.0:
+            vv = ("v", [lambda: g.vector.tensor_scalar(ap(o), ap(i), bias, None, OP.add)], tv)
+        else:
+            vv = ("v", [lambda: g.vector.tensor_scalar(ap(o), ap(i), scale, bias, OP.mult, OP.add)], tv)
+        op([o], [i], sv, vv)
 
     def mm(o, terms, start=True, stop=True):
         n = len(terms)
-        op("t", [o], [x for t in terms for x in t],
-           [lambda k=k: g.tensor.matmul(ap(o), ap(terms[k][0]), ap(terms[k][1]), start and k == 0, stop and k == n - 1)
-            for k in range(n)],
-           sum(max(64, num(t[1])) for t in terms) * CY * (4 if SCRATCH[terms[0][0][0]][2] == "float32" else 1))
+        op([o], [x for t in terms for x in t],
+           ("t", [lambda k=k: g.tensor.matmul(ap(o), ap(terms[k][0]), ap(terms[k][1]), start and k == 0,
+                                              stop and k == n - 1) for k in range(n)],
+            sum(max(64, num(t[1])) * (4 if SCRATCH[t[0][0]][2] == "float32" else 1) + 25 for t in terms) * PCY))
 
     def asel(o, i, pat, cmp, base, cm):
-        op("g", [o], [i], [lambda: g.affine_select(ap(o), ap(i), pat, cmp, 0.0, base, cm)], 0.17 + 2 * CY * num(o))
+        op([o], [i], ("g", [lambda: g.affine_select(ap(o), ap(i), pat, cmp, 0.0, base, cm)], 0.17 + 2 * CY * num(o)))
 
     def iota(o, pat, base, cm):
         if SCRATCH[o[0]][2] == "int32":
-            op("g", [o], [], [lambda: g.iota(ap(o), pat, base, cm)], 0.13 + 2 * CY * num(o))
+            op([o], [], ("g", [lambda: g.iota(ap(o), pat, base, cm)], 0.13 + 2 * CY * num(o)))
         else:
-            op("g", [o], [], [lambda: g.iota(ap(o), pat, base, cm, allow_small_or_imprecise_dtypes=True)],
-               0.13 + 2 * CY * num(o))
+            op([o], [], ("g", [lambda: g.iota(ap(o), pat, base, cm, allow_small_or_imprecise_dtypes=True)],
+                         0.13 + 2 * CY * num(o)))
 
     def dma(o_ap, i_ap, outs, ins):
         def emit():
@@ -231,7 +257,7 @@ def rank_program(g, core, T, topo):
             ndma[0] += 1
             g.sync.dma_start(o_ap, i_ap).then_inc(T.sem[s], 16)
             note("y", s, 16, outs, ins)
-        prog.append(("y", outs, ins, 0.1, emit, 2.5, first[0]))
+        prog.append(([("y", 0.1, emit)], outs, ins, 2.5, first[0]))
 
     peers = {d: T.cores[(rank + d) % N] for d in (1, 2, 3)}
     homes = {d: T.cores[(rank - d) % N] for d in (1, 2, 3)}
@@ -263,7 +289,7 @@ def rank_program(g, core, T, topo):
         def emit():
             need("g", guard, ins)
             g.remote_dma_fused(tr, local_sem=T.sem["loc"])
-        prog.append(("g", guard + [("sent" + sems, 0, 1, 1)], ins, 1.0, emit, None, first[0]))
+        prog.append(([("g", 1.0, emit)], guard + [("sent" + sems, 0, 1, 1)], ins, None, first[0]))
 
     def recv(sems, frm, pieces):
         for d in (1, 2, 3):
@@ -273,16 +299,16 @@ def rank_program(g, core, T, topo):
             c = (d - 1) * B
             ro = [R(nm, cc + c, cc + c + B) for nm, cc in pieces]
             arrived[sems + str(d)] = n
-            prog.append(("a", ro, [("sent" + sems, 0, 1, 1)], 0.0,
-                         lambda d=d, n=n, ro=ro: note(None, sems + str(d), n, ro, []), 5.0, 0.0))
+            prog.append(([("a", 0.0, lambda d=d, n=n, ro=ro: note(None, sems + str(d), n, ro, []))],
+                         ro, [("sent" + sems, 0, 1, 1)], 5.0, 0.0))
 
-    rings = {"f": [0, NF], "q": [0, 2], "t": [0, NT]}
+    turn = {r: 0 for r in RINGS}
     pools = {"a": [0, 1, 2], "c": [0, 1, 2, 4, 5, 6, 7], "z": [0, 1, 2, 3, 4, 5, 6, 7]}
     pool, pr = ["c"], [0]
 
     def ring(c):
-        rings[c][0] = (rings[c][0] + 1) % rings[c][1]
-        return "%s%d" % (c, rings[c][0])
+        turn[c] = (turn[c] + 1) % RINGS[c][0]
+        return "%s%d" % (c, turn[c])
 
     def F(n=512):
         return R(ring("f"), 0, n)
@@ -299,24 +325,68 @@ def rank_program(g, core, T, topo):
     LSA = R("ls", 0, 24)
     THR = R("th32", 0, 1)
     XA, KEY = R("xa", 0, W), R("key", 0, W)
+    ONE = R("one", 0, 512)
 
-    dma(T.x0i[:, 0:2048], T.x0[:], [R("x0i", 0, 2048)], [])
+    def M(name):
+        return R(name, 0, 128)
+
+    def shifted(name, k):
+        return R(name, 16 - k, 144 - k)
+
+    def lists(wf, ln):
+        pb = PQ(304)
+        for h in (0, 1):
+            mm(R(pb[0], 152 * h, 152 * h + 152), [(M("pm%d%d" % (h, c)), R(wf, c, 304, 2)) for c in (0, 1)])
+        vts(R(ln, 0, 304), pb, MG, OP.add, -MG, OP.add)
+
+    def wrap(flat, wf, lp, ln, rows="wz"):
+        pb = PQ(304)
+        mm(pb, [(shifted(rows, i), R(flat, i, P2, 16)) for i in range(16)])
+        sact(R(wf, 0, 304), pb, AF.Identity, bias=-0.5)
+        vcopy(R(lp, 0, 304), pb)
+        lists(wf, ln)
+
+    def partners(wf, dn, dp):
+        pb = PQ(256)
+        mm(pb, [(M("swp"), R(wf, 0, 256))])
+        vtt(R(dn, 0, 256), pb, R(wf, 0, 256), OP.subtract)
+        vtt(R(dp, 0, 256), R(wf, 0, 256), R("pih", 0, 256), OP.subtract)
+
+    def lst(l, c, h, k):
+        return R("l%d%s" % (l, c), 152 * h + CH[k][0] // 16, 152 * h + CH[k][1] // 16)
+
+    def pc(n, h, k):
+        a, b = CH[k]
+        o = V * h if k < 4 else V + GH * h
+        return R(n, o + a, o + b)
+
+    def chain(l, k, win, f, q, bias=0.0):
+        lin(q, IND(win, lst(l, "n", 0, k)), bias=bias)
+        for c, h in (("n", 1), ("p", 0), ("p", 1)):
+            vtt(q, IND(win, lst(l, c, h, k)), q, f)
+
+    for k in range(2):
+        dma(T.x0i[:, 1024 * k:1024 * k + 1024], T.x0[:, 1024 * k:1024 * k + 1024], [R("x0i", 1024 * k, 1024 * k + 1024)], [])
     dma(T.x0i[:, 2352:2376], T.shw[:], [R("x0i", 2352, 2376)], [])
     dma(T.x0i[:, 2048:2352], T.nxt[:], [R("x0i", 2048, 2352)], [])
     dma(T.x0i[:, 2376:2377], T.th[:], [R("x0i", 2376, 2377)], [])
     iota(R("pci", 0, 1), [[0, 1]], 0, 1)
     iota(R("t0", 0, 512), [[64, 8], [0, 64]], 0, 0)
     iota(R("t1", 0, 512), [[0, 8], [1, 64]], 0, 0)
-    vset(R("one", 0, 1024), 1.0)
-    vset(R("blk", 0, 128), 1.0)
-    vset(R("sel", 0, 128), 1.0)
-    vset(R("unh", 0, 2048), 0.0)
-    vset(R("unl", 0, 2048), 0.0)
-    asel(R("sel", 0, 128), R("sel", 0, 128), [[-16, 8], [0, 16]], OP.is_ge, 0, 1)
-    asel(R("sel", 0, 128), R("sel", 0, 128), [[16, 8], [0, 16]], OP.is_ge, 1, -1)
-    asel(R("blk", 0, 128), R("blk", 0, 128), [[-16, 8], [0, 16]], OP.is_ge, 0, 1)
-    asel(R("blk", 0, 128), R("blk", 0, 128), [[16, 8], [0, 16]], OP.is_ge, 15, -1)
-    asel(R("idn", 0, 128), R("one", 0, 128), [[-1, 128]], OP.is_equal, 0, 1)
+    vset(ONE, 1.0)
+    for n in ("blk", "sel", "seq"):
+        vset(M(n), 1.0)
+    vset(M("hlf"), 0.5)
+    vset(R("un", 0, 2052), 0.0)
+    for n in ("wz", "wq", "rz", "rn"):
+        vset(R(n, 0, 144), 0.0)
+    for n, lo, hi in (("sel", 0, 1), ("seq", 2, 3), ("blk", 0, 15)):
+        asel(M(n), M(n), [[-16, 8], [0, 16]], OP.is_ge, -lo, 1)
+        asel(M(n), M(n), [[16, 8], [0, 16]], OP.is_ge, hi, -1)
+    asel(M("idn"), R("one", 0, 128), [[-1, 128]], OP.is_equal, 0, 1)
+    for h in (0, 1):
+        for c in (0, 1):
+            asel(M("pm%d%d" % (h, c)), M("hlf"), [[-16, 8], [1000, 2], [-2, 8]], OP.is_equal, -h - 1000 * c, 1)
     vts(R("pci", 1, 2), R("pci", 0, 1), 1, OP.bitwise_and)
     vts(R("pci", 2, 3), R("pci", 0, 1), 15, OP.bitwise_and)
     vcopy(R("col", 0, 1), R("pci", 1, 2))
@@ -331,83 +401,48 @@ def rank_program(g, core, T, topo):
     vcopy(R("ls", 0, 24), R("x0i", 2352, 2376))
     for k in range(2):
         vcopy(R("xa", 1024 * k, 1024 * k + 1024), R("x0i", 1024 * k, 1024 * k + 1024))
-    sact(R("sx", 0, GH), IND(R("xa", 0, V), LSA))
-    send(peers, [("sx", 0, "xa", V)], "ax1_", [R("sx", 0, GH)])
+    sact(R("bs", 0, GH), IND(R("xa", 0, V), LSA))
+    send(peers, [("bs", 0, "xa", V)], "ax1_", [R("bs", 0, GH)])
     recv("ax1_", homes, [("xa", V)])
     first[0] = 0.0
+    vcopy(R("nxf", 0, 304), R("x0i", 2048, 2352))
+    vts(R("nxf", 0, 304), R("nxf", 0, 304), -0.5, OP.add)
     vcopy(R("lpn", 0, 304), R("x0i", 2048, 2352))
     for b in range(1, 10):
         n = min(512, P2 - 512 * b)
         sact(R("phl", 512 * b, 512 * b + n), R("phl", 0, n), AF.Identity, bias=R("col", 2 + b, 3 + b))
-    vts(R("x0i", 0, 304), R("x0i", 2048, 2352), 1, OP.arith_shift_right)
-    vcopy(R("l1n", 0, 304), R("x0i", 0, 304))
+    lists("nxf", "l1n")
     vcopy(IND(R("pvh", 0, P2), R("lpn", 0, 256)), R("phl", 0, 4096))
     vcopy(IND(R("pvh", 0, P2), R("lpn", 256, 304)), R("phl", 4096, P2))
-    vset(R("wrp", 0, 2048), 0.0)
-    vset(R("rdp", 0, 1024), 0.0)
-    vset(R("rdn", 0, 1024), 0.0)
-    vset(R("swp", 0, 128), 1.0)
-    vset(R("qr", 0, 128), 3.0 / 1024.0)
+    vset(M("swp"), 1.0)
+    vset(M("qr"), 3.0 / 1024.0)
+    vset(M("mgc"), MG / 128.0)
     vset(R("nm", 0, V), 0.0)
     for d in (1, 2, 3):
         vcopy(IND(R("nm", 0, V), LSB[d]), R("one", 0, 128))
     vcopy(THR, R("x0i", 2376, 2377))
-    sact(R("neg", 0, 128), R("idn", 0, 128), scale=-1.0)
-    sact(R("ngq", 0, 128), R("idn", 0, 128), scale=-0.25)
-    sact(R("d25", 0, 128), R("idn", 0, 128), scale=33554432.0)
-    sact(R("blp", 0, 128), R("blk", 0, 128), scale=4096.0)
-    sact(R("bln", 0, 128), R("blk", 0, 128), scale=-4096.0)
+    for n, i, c in (("neg", "idn", -1.0), ("ngq", "idn", -0.25), ("d25", "idn", 33554432.0), ("blp", "blk", 4096.0),
+                    ("bln", "blk", -4096.0)):
+        sact(M(n), M(i), scale=c)
     sact(R("ghl", 0, 768), R("phl", 4096, P2))
-    for k in range(16):
-        sact(R("wrp", 129 * k, 128 * k + 128, 16), R("sel", k, 128, 16))
-    asel(R("unh", 0, 2048, 2), R("one", 0, 1024), [[-1, 16], [-16, 8], [0, 8]], OP.is_equal, 0, 1)
-    asel(R("unl", 1, 2048, 2), R("one", 0, 1024), [[-1, 16], [-16, 8], [0, 8]], OP.is_equal, 0, 1)
+    sact(R("wz", 16, 144, 16), R("sel", 0, 128, 16))
+    sact(R("wq", 16, 144, 16), R("seq", 0, 128, 16))
+    for h in (0, 1):
+        sact(R("rz", 16 + h, 144, 16), R("blk", h, 128, 16))
+        sact(R("rn", 16 + h, 144, 16), R("blk", h, 128, 16), scale=-1.0)
+    asel(R("un", 4, 2052, 4), ONE, [[-1, 16], [-16, 8], [0, 4]], OP.is_equal, 0, 1)
     asel(R("swp", 0, 128, 2), R("swp", 0, 128, 2), [[-2, 64]], OP.is_equal, -1, 1)
     asel(R("swp", 1, 128, 2), R("swp", 1, 128, 2), [[-2, 64]], OP.is_equal, 0, 1)
     iota(R("pid", 0, 304), [[16, 304]], 0, 0)
     vts(R("pid", 0, 304), R("pid", 0, 304), R("col", 2, 3), OP.add)
-    vcopy(R("nxf", 0, 304), R("x0i", 2048, 2352))
-    vcopy(R("idh", 0, 128), R("idn", 0, 128))
-    vcopy(R("neh", 0, 128), R("neg", 0, 128))
-    vcopy(R("nqh", 0, 128), R("ngq", 0, 128))
-
-    def wrap(flat, wf, lp, ln):
-        pb = PQ(304)
-        mm(pb, [(R("wrp", 128 * i, 128 * i + 128), R(flat, i, P2, 16)) for i in range(16)])
-        vcopy(R("x0i", 304, 608), pb)
-        sact(R(wf, 0, 304), pb)
-        vts(R("x0i", 608, 912), R("x0i", 304, 608), 1, OP.arith_shift_right)
-        vcopy(R(ln, 0, 304), R("x0i", 608, 912))
-        vcopy(R(lp, 0, 304), R("x0i", 304, 608))
-
-    def partners(wf, dn, dp):
-        pb = PQ(256)
-        mm(pb, [(R("swp", 0, 128), R(wf, 0, 256))])
-        vtt(R(dn, 0, 256), pb, R(wf, 0, 256), OP.subtract)
-        vtt(R(dp, 0, 256), R(wf, 0, 256), R("pid", 0, 256), OP.subtract)
-
-    def lst(l, c, k):
-        return R("l%d%s" % (l, c), CH[k][0] // 8, CH[k][1] // 8)
-
-    def gath(eng, o, win, off):
-        (sact if eng == "s" else vcopy)(o, IND(win, off))
-
-    def pairs(l, k, win, f, out, bias=0.0):
-        n = 2 * (CH[k][1] - CH[k][0])
-        qn = ring("q")
-        q = R(qn, 0, n)
-        sact(q, IND(win, lst(l, "n", k)), AF.Identity if bias else AF.Copy, bias=bias)
-        vtt(q, IND(win, lst(l, "p", k)), q, f)
-        vtt(out, R(qn, 0, n, 2), R(qn, 1, n, 2), f)
+    vts(R("pih", 0, 256), R("pid", 0, 256), -0.5, OP.add)
+    vcopy(M("idh"), M("idn"))
+    vcopy(M("neh"), M("neg"))
+    vcopy(M("nqh"), M("ngq"))
 
     for k in range(5):
-        a, b = CH[k]
-        gath("s", R("fnx", 2 * a, 2 * b), XA, lst(1, "n", k))
-    for i in range(8):
         for h in (0, 1):
-            m = 2 * i + h
-            sact(R("rdp", 128 * i + m, 128 * i + 128, 16), R("blk", m, 128, 16))
-            sact(R("rdn", 128 * i + m, 128 * i + 128, 16), R("blk", m, 128, 16), scale=-1.0)
+            lin(pc("fnx", h, k), IND(XA, lst(1, "n", h, k)))
     wrap("pvh", "pvf", "lpp", "l1p")
     partners("nxf", "dnn", "dpn")
     partners("pvf", "dnp", "dpp")
@@ -415,89 +450,89 @@ def rank_program(g, core, T, topo):
     for l in (1, 2, 3):
         LVn = "lv%d" % l
         srcs = {1: [("fpv", "fnx")], 2: [("ga", "gb")], 3: [("fpv", "fnx"), ("pvh", "nxh")]}[l]
-        I1, NI, NQ = [R(x, 0, 128) for x in (("idh", "neh", "nqh") if l == 2 else ("idn", "neg", "ngq"))]
+        I1, NI, NQ = [M(x) for x in (("idh", "neh", "nqh") if l == 2 else ("idn", "neg", "ngq"))]
         pool[0] = "a"
-        zb = {}
+        zb, tk = {}, {}
 
         def gathers(k):
             a, b = CH[k]
-            o = -2 * a if l == 2 and k == 4 else 0
-            a2, b2 = o + 2 * a, o + 2 * b
+            n = b - a
             fp, fn = srcs[0]
-            if l == 1:
-                gath("v" if k % 2 == 0 else "s", R(fp, a2, b2), XA, lst(1, "p", k))
-            else:
-                gath("v", R(fn, a2, b2), XA, lst(l, "n", k))
-                gath("v", R(fp, a2, b2), XA, lst(l, "p", k))
+            if l > 1:
+                for h in (0, 1):
+                    lin(pc(fn, h, k), IND(XA, lst(l, "n", h, k)))
+            for h in (0, 1):
+                lin(pc(fp, h, k), IND(XA, lst(l, "p", h, k)))
             if l == 3:
                 for s, c in (("nxh", "n"), ("pvh", "p")):
-                    sact(R(s, a2, b2), IND(R("phl", W, P2), lst(l, c, k)), AF.Identity, bias=-0.375)
-            zb[k] = R("p%d" % (4 + k), 0, 512) if k < 4 else PQ(b - a)
-            mm(zb[k], [(NQ, R(p[1], a2 + h, b2, 2)) for p in srcs for h in (0, 1)] +
-               ([(R("qr", 0, 128), R("one", 0, b - a))] if l < 3 else []), stop=False)
-            mm(zb[k], [(NQ, R(p[0], a2 + h, b2, 2)) for p in srcs for h in (0, 1)], start=False)
+                    for h in (0, 1):
+                        lin(pc(s, h, k), IND(R("phl", W, P2), lst(l, c, h, k)), bias=-0.375)
+            zb[k] = R("p%d" % (4 + k), 0, 512) if k < 4 else PQ(n)
+            one = R("one", 0, n)
+            mm(zb[k], [(NQ, pc(p[1], h, k)) for p in srcs for h in (0, 1)] + ([(M("qr"), one)] if l < 3 else []), stop=False)
+            mm(zb[k], [(NQ, pc(p[0], h, k)) for p in srcs for h in (0, 1)] + [(M("mgc"), one)], start=False)
+            xm = F(n)
+            lin(xm, R("xa", a, b), bias=-MG)
+            vtt(zb[k], zb[k], xm, OP.add)
+
+        def sized(k):
+            return [(M("sel"), R("phl", CH[k][0], CH[k][1])), (M("blp" if l == 1 else "bln"), tk[k])]
 
         def detail(k):
             a, b = CH[k]
-            n = b - a
-            xm = F(n)
-            sact(xm, R("xa", a, b), AF.Identity, bias=-MG)
-            sact(zb[k], zb[k], AF.Identity, bias=MG)
-            d, e = (R("dd", a, b), R("ad", a, b)) if k < 4 else (F(n), F(n))
-            vtt(d, zb[k], xm, OP.add)
-            sact(e, d, AF.Abs)
-            t = R(ring("t"), 0, n)
+            n, d = b - a, zb[k]
+            t = e = tk[k] = R("tk", a, b) if k < 4 else R(ring("t"), 0, n)
             if l == 1:
-                sact(t, e)
+                sact(t, d, AF.Abs)
             else:
+                e = F(n)
+                sact(e, d, AF.Abs)
                 sact(t, e, AF.Relu, bias=255.0, scale=-1.0)
-            terms = [(R("sel", 0, 128), R("phl", a, b)), (R("blp" if l == 1 else "bln", 0, 128), t)]
-            mm(zb[k], terms)
-            sact(R("key", a, b), zb[k])
-            if k < 4:
-                mm(zb[k], [(R("d25", 0, 128), R(x, a, b)) for x in ["nm"] + ["lv%d" % j for j in range(1, l)]] + terms)
-
-        def pack(k):
-            a, b = CH[k]
-            d, e = R("dd", a, b), R("ad", a, b)
-            q, w = F(), F()
-            m, ds = PQ(), PQ()
-            sact(q, d, AF.Identity, bias=-0.375, scale=0.25)
-            sact(q, q, AF.Identity, bias=MG)
-            sact(ds, q, AF.Identity, bias=-MG)
+            o = PQ(n)
+            mm(o, sized(k))
+            lin(R("key", a, b), o)
+            if k == 4:
+                return
+            m, w, q, ds = R(ring("m"), 0, 512), F(), F(), PQ()
             vts(m, e, THR, OP.is_ge)
             if l < 3:
-                sact(w, m, AF.Identity, bias=KP)
+                lin(w, m, bias=KP)
             else:
-                sact(w, m, AF.Identity, bias=1.0, scale=-1.0)
-            vtt(d, m, d, OP.mult)
-            vtt(e, ds, w, OP.mult)
+                lin(w, m, -1.0, 1.0)
+            lin(q, d, 0.25, -0.375)
+            vtt(R("dd", a, b), d, m, OP.mult)
+            vts(ds, q, MG, OP.add, -MG, OP.add)
+            vtt(d, ds, w, OP.mult)
 
         def chosen(k):
             a, b = CH[k]
-            f = F()
-            pairs(l, k, KEY, OP.min, f)
-            vtt(R(LVn, a, b), zb[k], f, OP.is_lt)
+            f = R(ring("q"), 0, 512)
+            chain(l, k, KEY, OP.min, f)
+            o = PQ()
+            mm(o, [(M("d25"), R(x, a, b)) for x in ["nm"] + ["lv%d" % j for j in range(1, l)]] + sized(k))
+            vtt(R(LVn, a, b), o, f, OP.is_lt)
 
         def likeness(k):
-            a, b = CH[k]
             terms = []
-            for x, y, sg in ((0, 0, "rdp"), (1, 1, "rdp"), (0, 1, "rdn"), (1, 0, "rdn")):
+            for x, y in ((0, 0), (1, 1), (0, 1), (1, 0)):
                 u = PQ()
-                mm(u, [(I1, R(s[0], 2 * a + x, 2 * b, 2)) for s in srcs] + [(NI, R(s[1], 2 * a + y, 2 * b, 2)) for s in srcs])
+                mm(u, [(I1, pc(s[0], x, k)) for s in srcs] + [(NI, pc(s[1], y, k)) for s in srcs])
                 tn = ring("t")
-                sact(R(tn, 0, 512), u, AF.Abs)
-                if l > 1:
-                    vts(R(tn, 0, 512), R(tn, 0, 512), 255.0, OP.min)
-                terms += [(R(sg, 128 * i, 128 * i + 128), R(tn, i, 512, 8)) for i in range(8)]
+                if l == 1:
+                    lin(R(tn, 0, 512), u, relu=True)
+                else:
+                    sact(R(tn, 0, 512), u, AF.Abs)
+                    sact(R(tn, 0, 512), R(tn, 0, 512), AF.Relu, bias=255.0, scale=-1.0)
+                sg = "rz" if (x == y) == (l == 1) else "rn"
+                terms += [(shifted(sg, 2 * i), R(tn, i, 512, 8)) for i in range(8)]
             mm(R("p3", 64 * k, 64 * k + 64), terms)
 
         def links_small():
             lb = PB()
             for k in range(4):
                 a, b = CH[k]
-                mm(R(lb, 64 * k, 64 * k + 64), [(R("rdp", 128 * i, 128 * i + 128), R(LVn, a + i, b, 8)) for i in range(8)])
-            sact(R("lw", 0, 256), R(lb, 0, 256), scale=1.0 / 16)
+                mm(R(lb, 64 * k, 64 * k + 64), [(shifted("rz", 2 * i), R(LVn, a + i, b, 8)) for i in range(8)])
+            lin(R("lw", 0, 256), R(lb, 0, 256), 1.0 / 16)
             vts(R("lc", 0, 256), R("p3", 0, 256), 0.0, OP.is_gt)
             vtt(R("lc", 0, 256), R("lc", 0, 256), R("lw", 0, 256), OP.mult)
             for (dn, dp, h, lo) in (("dnn", "dpn", "hn", "ln_"), ("dnp", "dpp", "hp", "lp_"))[:2 if l < 3 else 1]:
@@ -505,36 +540,38 @@ def rank_program(g, core, T, topo):
                 vtt(R("w1", 0, 256), R("lw", 0, 256), R(dp, 0, 256), OP.mult)
                 vtt(R("w0", 0, 256), R("w0", 0, 256), R("w1", 0, 256), OP.add)
                 vtt(R("w0", 0, 256), R("w0", 0, 256), R("pid", 0, 256), OP.add)
-                sact(R(h, 0, 256), R("w0", 0, 256))
+                lin(R(h, 0, 256), R("w0", 0, 256))
                 vtt(R(lo, 0, 256), R("w0", 0, 256), R(h, 0, 256), OP.subtract)
 
-        def unwrap(fn, h, lo):
+        def unwrap():
             if l != 2:
-                sact(R(fn, 4096, P2), R("ghl", 0, 768))
+                lin(R("fnx", 4096, P2), R("ghl", 0, 768))
             for i in range(16):
                 if i % 2 == 0:
                     bn = PB()
                 bk = R(bn, 256 * (i % 2), 256 * (i % 2) + 256)
-                mm(bk, [(R("unh", 128 * i, 128 * i + 128), R(h, 0, 256)), (R("unl", 128 * i, 128 * i + 128), R(lo, 0, 256))])
-                sact(R(fn, i, 4096, 16), bk)
+                mm(bk, [(R("un", 4 + 128 * i - r, 132 + 128 * i - r), R(x, 0, 256))
+                        for r, x in enumerate(("hn", "ln_", "hp", "lp_")[:4 if l < 3 else 2])])
+                lin(R("fnx", i, 4096, 16), bk)
 
         def own(k):
             a, b = CH[k]
             x, b1, b2 = R("xa", a, b), PQ(), PQ()
             if l < 3:
                 s = R("sp%d" % l, a, b)
-                pairs(l, k, KEY, OP.add, s)
+                chain(l, k, KEY, OP.add, s)
                 z = F()
-                sact(z, s, AF.Identity, bias=MG * KP)
-                sact(b1, z, AF.Identity, bias=-MG, scale=1.0 / KP)
-                sact(b2, z, AF.Identity, bias=-MG * KP)
+                lin(z, s, bias=MG * KP)
+                lin(b1, z, 1.0 / KP, -MG)
+                lin(b2, z, bias=-MG * KP)
                 vtt(x, b1, x, OP.add)
                 vtt(s, s, b2, OP.subtract)
             else:
-                sact(b2, R(LVn, a, b), scale=-BIG)
+                q = R(ring("q"), 0, 512)
+                lin(b2, R(LVn, a, b), -BIG)
                 vtt(x, b2, x, OP.add)
-                pairs(l, k, KEY, OP.add, b1)
-                vtt(x, b1, x, OP.add)
+                chain(l, k, KEY, OP.add, q)
+                vtt(x, q, x, OP.add)
 
         def border(buf, rc):
             for d in (1, 2, 3):
@@ -544,20 +581,19 @@ def rank_program(g, core, T, topo):
 
         def kept(k):
             a, b = CH[k]
-            f, b1, b2 = F(), PQ(), PQ()
-            sact(b2, R("dd", a, b), AF.Identity, bias=BIG)
-            vtt(f, b2, R(LVn, a, b), OP.mult)
-            sact(R("dd" if l == 3 else "dl%d" % l, a, b), f, AF.Identity, bias=-BIG if l == 1 else -(BIG + MG))
+            b2 = PQ()
+            lin(b2, R(LVn, a, b), BIG, -(BIG + MG))
+            vtt(R("dd" if l == 3 else "dl%d" % l, a, b), b2, R("dd", a, b), OP.add)
             if l < 3:
-                s = R("sp%d" % l, a, b)
-                sact(b1, R(LVn, a, b), scale=BIG)
+                b1, s = PQ(), R("sp%d" % l, a, b)
+                lin(b1, R(LVn, a, b), BIG)
                 vtt(s, b1, s, OP.add)
 
         if l == 3:
             for k in range(5):
                 a, b = CH[k]
                 t = R(ring("t"), 0, b - a)
-                sact(t, R("xa", a, b))
+                lin(t, R("xa", a, b))
                 vtt(R("phl", W + a, W + b), R("xa", a, b), t, OP.subtract)
         order = [4, 0, 1, 2, 3] if l > 1 else [0, 1, 2, 3, 4]
         for i in range(6):
@@ -565,56 +601,50 @@ def rank_program(g, core, T, topo):
                 gathers(order[i])
             if i > 0:
                 detail(order[i - 1])
-        for k in (0, 1):
-            pack(k)
         for k in range(4):
             chosen(k)
-            if k < 2:
-                pack(k + 2)
             if k < (4 if l < 3 else 2):
                 likeness(k)
-        pool[0] = "c"
         vset(R("key", V, W), 0.0)
         for k in range(4):
             a, b = CH[k]
-            vtt(R("key", a, b), R("ad", a, b), R(LVn, a, b), OP.mult)
+            vtt(R("key", a, b), zb[k], R(LVn, a, b), OP.mult)
+        pool[0] = "c"
         rs = "rs2" if l == 2 else "rs1"
         xg = [R("xa", V, W)]
         if l < 3:
             q, z, b4 = F(GH), F(GH), PQ(GH)
-            pairs(l, 4, KEY, OP.add, q)
-            sact(z, q, AF.Identity, bias=MG * KP)
-            sact(b4, z, AF.Identity, bias=-MG * KP)
-            sact(R("ss", 0, GH), z, AF.Identity, bias=-MG, scale=1.0 / KP)
+            chain(l, 4, KEY, OP.add, q)
+            lin(z, q, bias=MG * KP)
+            lin(b4, z, bias=-MG * KP)
+            lin(R("ss", 0, GH), z, 1.0 / KP, -MG)
             vtt(R("ss", GH, 768), q, b4, OP.subtract)
             send(homes, [("ss", 0, rs, 0), ("ss", GH, rs, GH)], "as%d_" % l, [R("ss", 0, 768)], xg)
             recv("as%d_" % l, peers, [(rs, 0), (rs, GH)])
             links_small()
             own(0)
             own(1)
-            unwrap("fnx", "hn", "ln_")
+            unwrap()
             own(2)
             own(3)
             border("xa", 0)
-            sact(R("sx", 0, GH), IND(R("xa", 0, V), LSA))
-            send(peers, [("sx", 0, "xa", V)], "ax%d_" % (l + 1), [R("sx", 0, GH)], [R("rs1", 0, 768)] if l == 2 else [])
+            sact(R("bs", 0, GH), IND(R("xa", 0, V), LSA))
+            send(peers, [("bs", 0, "xa", V)], "ax%d_" % (l + 1), [R("bs", 0, GH)], [R("rs1", 0, 768)] if l == 2 else [])
             recv("ax%d_" % (l + 1), homes, [("xa", V)])
-            unwrap("fpv", "hp", "lp_")
-            gath("v", R("nxh", 0, 4096), R("fnx", 0, P2), R("lpn", 0, 256))
-            gath("s", R("nxh", 4096, P2), R("fnx", 0, P2), R("lpn", 256, 304))
-            gath("s", R("pvh", 0, 3584), R("fpv", 0, P2), R("lpp", 0, 224))
-            gath("v", R("pvh", 3584, P2), R("fpv", 0, P2), R("lpp", 224, 304))
+            for (o, lp) in (("nxh", "lpn"), ("pvh", "lpp")):
+                for k in range(4):
+                    lin(R(o, 1216 * k, 1216 * k + 1216), IND(R("fnx", 0, P2), R(lp, 76 * k, 76 * k + 76)))
             wrap("nxh", "nxf", "lpn", "l%dn" % (l + 1))
             border("sp%d" % l, GH)
             sact(R("sg%d" % l, 0, GH), IND(R("sp%d" % l, 0, V), LSA))
             for k in range(4):
                 kept(k)
-            wrap("pvh", "pvf", "lpp", "l%dp" % (l + 1))
+            wrap("pvh", "pvf", "lpp", "l%dp" % (l + 1), "wq")
             partners("nxf", "dnn", "dpn")
             if l < 2:
                 partners("pvf", "dnp", "dpp")
         else:
-            pairs(l, 4, KEY, OP.add, R("ss", 0, GH))
+            chain(l, 4, KEY, OP.add, R("ss", 0, GH))
             send(homes, [("ss", 0, rs, 0)], "as3_", [R("ss", 0, GH)], xg)
             recv("as3_", peers, [(rs, 0)])
             for k in range(4):
@@ -633,7 +663,7 @@ def rank_program(g, core, T, topo):
             likeness(2)
             likeness(3)
             links_small()
-            unwrap("fnx", "hn", "ln_")
+            unwrap()
 
     pool[0] = "z"
 
@@ -641,9 +671,9 @@ def rank_program(g, core, T, topo):
         fms = {}
         for k in range(5):
             if k < 4:
-                z, fms[k] = PQ(), PQ()
-                pairs(l, k, R(src, 0, W), OP.add, z, -0.75)
-                sact(fms[k], z, AF.Identity, bias=MG, scale=0.25)
+                z, fms[k] = R(ring("q"), 0, 512), PQ()
+                chain(l, k, R(src, 0, W), OP.add, z, -1.5)
+                lin(fms[k], z, 0.25, MG)
             if k > 0:
                 a, b = CH[k - 1]
                 y, mx = PQ(), PQ()
@@ -656,28 +686,25 @@ def rank_program(g, core, T, topo):
                     vtt(R(dst, a, b), mx, R(sp, a, b), OP.subtract)
 
     undo(3, "xa", "key", "dd", "sp2")
-    for k in range(4):
-        a, b = CH[k]
-        sact(R("sp2", a, b), R("dl1", a, b), AF.Identity, bias=-MG)
     sact(R("xa", V, W), R("rb1", 0, GH))
-    gath("v", R("nxh", 0, 2432), R("fnx", 0, P2), R("lpn", 0, 152))
-    gath("s", R("nxh", 2432, P2), R("fnx", 0, P2), R("lpn", 152, 304))
+    for k in range(4):
+        lin(R("nxh", 1216 * k, 1216 * k + 1216), IND(R("fnx", 0, P2), R("lpn", 76 * k, 76 * k + 76)))
     undo(2, "key", "xa", "dl2", "sp1")
     for k in range(10):
         a, b = 512 * k, min(512 * k + 512, P2)
         bk = PQ(b - a)
-        mm(bk, [(R("sel", 0, 128), R("nxh", a, b))])
-        o = R("dd", a, b) if k < 4 else R("ad", a - V, b - V) if k < 8 else R("f%d" % (k - 8), 0, b - a)
-        sact(o, bk)
+        mm(bk, [(M("sel"), R("nxh", a, b))])
+        o = R("dd", a, b) if k < 4 else R("sp2", a - V, b - V) if k < 8 else R("f%d" % (k - 8), 0, b - a)
+        lin(o, bk)
         if k == 3 or k == 7:
-            nm = "dd" if k == 3 else "ad"
+            nm = "dd" if k == 3 else "sp2"
             dma(T.yn[:, b - V:b], T[nm][0:128:16, 0:V], [], [R(nm, 0, V)])
         if k >= 8:
             dma(T.yn[:, a:b], T[o[0]][0:128:16, 0:b - a], [], [o])
-    undo(1, "xa", "key", "sp2", None)
+    undo(1, "xa", "key", "dl1", None)
 
-    for i in ordered(prog):
-        prog[i][4]()
+    for emit in ordered(prog):
+        emit()
 
     for e in ("v", "s", "t", "g"):
         g.wait_ge(T.sem[semof[e]], tick[e])

from concourse.bass import DstId, RemoteDMATransfer
from concourse.mybir import AluOpType as OP, ActivationFunctionType as AF

V, B, W, P2 = 2048, 128, 2432, 4864
GH = 384
MG = 12582912.0
KP = 4096.0
BIG = 1048576.0

TU = {"CY": 0.0009, "PCY": 0.0006, "WK": 0.1, "OV": 0.05, "GA": 1.4, "TT": 1.8, "VPEN": 0.6}
SCRATCH = {}
for _n, _c, _t in (
        ("xa", W, "float32"), ("key", W, "float32"), ("dd", V, "float32"),
        ("sp1", V, "float32"), ("sp2", V, "float32"), ("dl1", V, "float32"), ("dl2", V, "float32"),
        ("ga", P2, "float16"), ("gb", P2, "float16"), ("fnx", P2, "bfloat16"), ("fpv", P2, "bfloat16"),
        ("nxh", P2, "bfloat16"), ("pvh", P2, "bfloat16"), ("phl", P2, "bfloat16"), ("ghl", 768, "bfloat16"),
        ("lv1", V, "bfloat16"), ("lv2", V, "bfloat16"), ("lv3", V, "bfloat16"), ("nm", V, "bfloat16"),
        ("tk", V, "bfloat16"), ("un", 2052, "bfloat16"), ("wz", 144, "bfloat16"), ("wq", 144, "bfloat16"),
        ("rz", 144, "bfloat16"), ("rn", 144, "bfloat16"),
        ("idn", 128, "bfloat16"), ("neg", 128, "bfloat16"), ("ngq", 128, "bfloat16"), ("d25", 128, "bfloat16"),
        ("blk", 128, "bfloat16"), ("blp", 128, "bfloat16"), ("bln", 128, "bfloat16"), ("sel", 128, "bfloat16"),
        ("seq", 128, "bfloat16"), ("mgc", 128, "bfloat16"),
        ("idh", 128, "float16"), ("neh", 128, "float16"), ("nqh", 128, "float16"),
        ("qr", 128, "bfloat16"), ("swp", 128, "float32"), ("one", 512, "bfloat16"), ("hlf", 128, "float32"),
        ("pm00", 128, "float32"), ("pm01", 128, "float32"), ("pm10", 128, "float32"), ("pm11", 128, "float32"),
        ("x0i", 2380, "int32"), ("pci", 8, "int32"), ("col", 16, "float32"), ("th32", 8, "float32"), ("ls", 24, "uint16"),
        ("pid", 304, "float32"), ("pih", 256, "float32"), ("nxf", 304, "float32"), ("pvf", 304, "float32"),
        ("dnn", 256, "float32"), ("dnp", 256, "float32"), ("dpn", 256, "float32"), ("dpp", 256, "float32"),
        ("lw", 256, "float32"), ("lc", 256, "float32"), ("w0", 256, "float32"), ("w1", 256, "float32"),
        ("hn", 256, "bfloat16"), ("hp", 256, "bfloat16"), ("ln_", 256, "bfloat16"), ("lp_", 256, "bfloat16"),
        ("lpn", 304, "uint16"), ("lpp", 304, "uint16"),
        ("ss", 768, "float32"), ("rs1", 768, "float32"), ("rs2", 768, "float32"),
        ("bs", 3 * GH, "float32"), ("rb1", GH, "float32"), ("rb2", GH, "float32"),
        ("sg1", GH, "float32"), ("sg2", GH, "float32"), ("bt", 128, "float32")):
    SCRATCH[_n] = ("sbuf", [128, _c], _t)
RINGS = {"f": (6, "float32"), "q": (4, "float32"), "t": (6, "bfloat16"), "m": (2, "bfloat16")}
for _r in RINGS:
    for _k in range(RINGS[_r][0]):
        SCRATCH["%s%d" % (_r, _k)] = ("sbuf", [128, 512], RINGS[_r][1])
for _k in range(8):
    SCRATCH["p%d" % _k] = ("psum", [128, 512], "float32")
for _k in (1, 2, 3):
    SCRATCH["l%dn" % _k] = ("sbuf", [128, 304], "uint16")
    SCRATCH["l%dp" % _k] = ("sbuf", [128, 304], "uint16")
ARR = [a + str(d) for a in ("ax1_", "ax2_", "ax3_", "as1_", "as2_", "as3_", "ab3_", "ab2_") for d in (1, 2, 3)]
SEMAPHORES = ["sv", "ss_", "st", "sg", "loc"] + ARR + ["d%d" % k for k in range(20)]
PSUMS = ["p%d" % k for k in range(8)]


def R(name, a, b, s=1):
    return (name, a, b, s)


def IND(win, off):
    return ("ind", win, off)


def hits(x, y):
    if x[0] >= y[1] or y[0] >= x[1]:
        return False
    return not (x[2] == y[2] and x[2] > 1 and (x[0] - y[0]) % x[2])


def ordered(prog):
    n, WK = len(prog), TU["WK"]
    preds, succs = [set() for _ in range(n)], [set() for _ in range(n)]
    acc = {}
    for i, (var, ro, ri, lat, up) in enumerate(prog):
        e = var[0][0] if len(var) == 1 else None
        for lst, wr in ((ro, True), (ri, False)):
            for (nm, a, b, s) in lst:
                ps = nm in PSUMS
                for (j, e2, a2, b2, s2, w2) in acc.get(nm, ()):
                    if j != i and ((ps and (e is None or e != e2)) or ((wr or w2) and hits((a, b, s), (a2, b2, s2)))):
                        preds[i].add(j)
        for lst, wr in ((ro, True), (ri, False)):
            for (nm, a, b, s) in lst:
                old = acc.get(nm, [])
                if wr and s == 1:
                    old = [o for o in old if not (o[2] >= a and o[3] <= b and
                                                  (nm not in PSUMS or (e is not None and o[1] == e)))]
                acc[nm] = old + [(i, e, a, b, s, wr)]
    for i in range(n):
        for j in preds[i]:
            succs[j].add(i)
    dur = [min(v[1] for v in p[0]) + (p[3] or 0.0) for p in prog]
    tail = [0.0] * n
    for i in range(n - 1, -1, -1):
        tail[i] = prog[i][4] + dur[i] + max([tail[j] + WK for j in succs[i]] or [0.0])
    left = [len(p) for p in preds]
    ready = {i: 0.0 for i in range(n) if not left[i]}
    free, out, when = {}, [], [0.0] * n

    def start(i, r):
        return min(max(r, free.get(v[0], 0.0)) for v in prog[i][0])
    while ready:
        t = min(start(i, r) for i, r in ready.items())
        best = None
        for i, r in ready.items():
            if start(i, r) <= t + 0.02 and (best is None or (tail[i], -i) > (tail[best], -best)):
                best = i
        i = best
        r = ready.pop(i)
        var = min(prog[i][0], key=lambda v: max(r, free.get(v[0], 0.0)) + v[1] + (TU["VPEN"] if v[0] == "v" else 0.0))
        t = max(r, free.get(var[0], 0.0))
        if var[0] != "a":
            free[var[0]] = t + var[1]
        out.append(var[2])
        for j in succs[i]:
            when[j] = max(when[j], t + var[1] + (prog[i][3] or 0.0) + WK)
            left[j] -= 1
            if not left[j]:
                ready[j] = when[j]
    return out


def rank_program(g, core, T, topo):
    rank = T.rank_of(core)
    if rank is None:
        return
    N = len(T.cores)
    CY, PCY, GA = TU["CY"], TU["PCY"], TU["GA"]
    queues = {"v": g.vector, "s": g.scalar, "t": g.tensor, "g": g, "y": g.sync}
    semof = {"v": "sv", "s": "ss_", "t": "st", "g": "sg"}
    tick = {"v": 0, "s": 0, "t": 0, "g": 0}
    known = {e: {} for e in queues}
    snaps = {}
    acc = {}
    prog = []
    ndma, local, arrived = [0], [0], {}
    first = [0.0]

    def ap(v):
        if v[0] == "ind":
            return T[v[1][0]][:, v[1][1]:v[1][2]].indirect(T[v[2][0]][:, v[2][1]:v[2][2]])
        n, a, b, s = v
        return T[n][:, a:b] if s == 1 else T[n][:, a:b:s]

    def need(e, outs, ins):
        w = {}
        for lst, wr in ((outs, True), (ins, False)):
            for (n, a, b, s) in lst:
                for (src, cnt, a2, b2, s2, wr2) in acc.get(n, []):
                    if (src == e or n not in PSUMS) and (not (wr or wr2) or not hits((a, b, s), (a2, b2, s2))):
                        continue
                    w[src] = max(w.get(src, 0), cnt)
        k = known[e]
        w = {s: c for s, c in w.items() if k.get(s, 0) < c}
        for s, c in list(w.items()):
            if any(s2 != s and snaps[(s2, c2)].get(s, 0) >= c for s2, c2 in w.items()):
                w.pop(s)
        for s, c in w.items():
            queues[e].wait_ge(T.sem[semof.get(s, s)], c)
            for s2, c2 in [(s, c)] + list(snaps[(s, c)].items()):
                k[s2] = max(k.get(s2, 0), c2)

    def note(e, src, cnt, outs, ins):
        snaps[(src, cnt)] = dict(known[e]) if e else {}
        for lst, wr in ((outs, True), (ins, False)):
            for (n, a, b, s) in lst:
                old = acc.get(n, [])
                if wr and s == 1:
                    old = [o for o in old if not (o[2] >= a and o[3] <= b and (n not in PSUMS or o[0] == src))]
                else:
                    old = [o for o in old if not (o[0] == src and o[2:] == (a, b, s, wr))]
                acc[n] = old + [(src, cnt, a, b, s, wr)]

    def op(outs, ins, *variants):
        ro = [v[1] if v[0] == "ind" else v for v in outs]
        ri = [v[2] for v in outs if v[0] == "ind"]
        for v in ins:
            ri += [v[1], v[2]] if v[0] == "ind" else [v]

        def emitter(e, calls):
            def emit():
                need(e, ro, ri)
                for c in calls[:-1]:
                    c()
                tick[e] += 1
                calls[-1]().then_inc(T.sem[semof[e]], 1)
                note(e, e, tick[e], ro, ri)
            return emit
        prog.append(([(e, cost + TU["OV"], emitter(e, calls)) for e, calls, cost in variants], ro, ri, None, first[0]))

    def num(v):
        return 16 * (v[2][2] - v[2][1]) if v[0] == "ind" else (v[2] - v[1] + v[3] - 1) // v[3]

    def tm(n, *vs):
        two = all(SCRATCH[v[0]][2] in ("bfloat16", "float16") for v in vs)
        return CY * max(64, n * (0.5 if two else 1))

    def vcopy(o, i):
        n = num(i)
        op([o], [i], ("v", [lambda: g.vector.tensor_copy(ap(o), ap(i))],
                      3.8 * CY * n if o[0] == "ind" else GA * CY * n if i[0] == "ind" else tm(n, o, i)))

    def vtt(o, a, b, f):
        op([o], [a, b], ("v", [lambda: g.vector.tensor_tensor(ap(o), ap(a), ap(b), f)],
                         CY * max(64, num(b) * (1 if a[0] in PSUMS or b[0] in PSUMS else TU["TT"] if a[0] == "ind" else 2))))

    def vts(o, a, s1, f1, s2=None, f2=None):
        x1 = ap(s1) if isinstance(s1, tuple) else s1
        cols = [s1] if isinstance(s1, tuple) else []
        if f2 is None:
            op([o], [a] + cols, ("v", [lambda: g.vector.tensor_scalar(ap(o), ap(a), x1, None, f1)], tm(num(a), o, a)))
        else:
            op([o], [a] + cols, ("v", [lambda: g.vector.tensor_scalar(ap(o), ap(a), x1, s2, f1, f2)], tm(num(a), o, a)))

    def vset(o, c):
        op([o], [], ("v", [lambda: g.vector.memset(ap(o), c)], tm(num(o))))

    def sact(o, i, f=AF.Copy, bias=0.0, scale=1.0):
        n = num(i)
        col = isinstance(bias, tuple)
        bb = ap(bias) if col else bias
        op([o], [i] + ([bias] if col else []),
           ("s", [lambda: g.scalar.activation(ap(o), ap(i), f, bias=bb, scale=scale)],
            CY * (GA * n if i[0] == "ind" else max(64, n)) + 0.01))

    def lin(o, i, scale=1.0, bias=0.0, relu=False):
        n = num(i)
        ind = i[0] == "ind"
        sv = ("s", [lambda: g.scalar.activation(ap(o), ap(i), AF.Relu if relu else AF.Identity, bias=bias, scale=scale)],
              CY * (GA * n if ind else max(64, n)) + 0.01)
        tv = CY * GA * n if ind else tm(n, o, i)
        if relu:
            vv = ("v", [lambda: g.vector.tensor_scalar(ap(o), ap(i), 0.0, None, OP.max)], tv)
        elif scale == 1.0 and bias == 0.0:
            vv = ("v", [lambda: g.vector.tensor_copy(ap(o), ap(i))], tv)
        elif scale == 1.0:
            vv = ("v", [lambda: g.vector.tensor_scalar(ap(o), ap(i), bias, None, OP.add)], tv)
        else:
            vv = ("v", [lambda: g.vector.tensor_scalar(ap(o), ap(i), scale, bias, OP.mult, OP.add)], tv)
        op([o], [i], sv, vv)

    def mm(o, terms, start=True, stop=True):
        n = len(terms)
        op([o], [x for t in terms for x in t],
           ("t", [lambda k=k: g.tensor.matmul(ap(o), ap(terms[k][0]), ap(terms[k][1]), start and k == 0,
                                              stop and k == n - 1) for k in range(n)],
            sum(max(64, num(t[1])) * (4 if SCRATCH[t[0][0]][2] == "float32" else 1) + 25 for t in terms) * PCY))

    def asel(o, i, pat, cmp, base, cm):
        op([o], [i], ("g", [lambda: g.affine_select(ap(o), ap(i), pat, cmp, 0.0, base, cm)], 0.17 + 2 * CY * num(o)))

    def iota(o, pat, base, cm):
        if SCRATCH[o[0]][2] == "int32":
            op([o], [], ("g", [lambda: g.iota(ap(o), pat, base, cm)], 0.13 + 2 * CY * num(o)))
        else:
            op([o], [], ("g", [lambda: g.iota(ap(o), pat, base, cm, allow_small_or_imprecise_dtypes=True)],
                         0.13 + 2 * CY * num(o)))

    def dma(o_ap, i_ap, outs, ins):
        def emit():
            need("y", outs, ins)
            s = "d%d" % ndma[0]
            ndma[0] += 1
            g.sync.dma_start(o_ap, i_ap).then_inc(T.sem[s], 16)
            note("y", s, 16, outs, ins)
        prog.append(([("y", 0.1, emit)], outs, ins, 2.5, first[0]))

    peers = {d: T.cores[(rank + d) % N] for d in (1, 2, 3)}
    homes = {d: T.cores[(rank - d) % N] for d in (1, 2, 3)}

    def split(src, dsts):
        away = [c for c in dsts if topo.chip(c) != topo.chip(src)]
        pool = topo.engines(src, away[0])
        n = len(pool) // len(away)
        res = {c: pool[k * n:(k + 1) * n] for k, c in enumerate(away)}
        for c in dsts:
            if c not in res:
                res[c] = [e for e in topo.engines(src, c) if e not in pool]
        return res

    def send(to, pieces, sems, ins, guard=()):
        m = split(core, [to[d] for d in (1, 2, 3)])
        tr = []
        for d in (1, 2, 3):
            rid, pid, _ = topo.addr(to[d])
            n = len(m[to[d]]) // len(pieces)
            for k, (sn, sc, dn, dc) in enumerate(pieces):
                c = (d - 1) * B
                tr.append(RemoteDMATransfer(
                    dst_ids=[DstId(rid=rid, pnc=pid)], dma_engine_mask=sum(1 << e for e in m[to[d]][k * n:(k + 1) * n]),
                    remote_sem=T.sem[sems + str(d)], src=T[sn][:, sc + c:sc + c + B], dst=T[dn][:, dc + c:dc + c + B]))
                local[0] += n
        guard = list(guard)

        def emit():
            need("g", guard, ins)
            g.remote_dma_fused(tr, local_sem=T.sem["loc"])
        prog.append(([("g", 1.0, emit)], guard + [("sent" + sems, 0, 1, 1)], ins, None, first[0]))

    def recv(sems, frm, pieces):
        for d in (1, 2, 3):
            r = T.rank_of(frm[d])
            s = 1 if frm is homes else -1
            n = len(split(frm[d], [T.cores[(r + s * j) % N] for j in (1, 2, 3)])[core]) // len(pieces) * len(pieces)
            c = (d - 1) * B
            ro = [R(nm, cc + c, cc + c + B) for nm, cc in pieces]
            arrived[sems + str(d)] = n
            prog.append(([("a", 0.0, lambda d=d, n=n, ro=ro: note(None, sems + str(d), n, ro, []))],
                         ro, [("sent" + sems, 0, 1, 1)], 5.0, 0.0))

    turn = {r: 0 for r in RINGS}
    pools = {"a": [0, 1, 2], "c": [0, 1, 2, 4, 5, 6, 7], "z": [0, 1, 2, 3, 4, 5, 6, 7]}
    pool, pr = ["c"], [0]

    def ring(c):
        turn[c] = (turn[c] + 1) % RINGS[c][0]
        return "%s%d" % (c, turn[c])

    def F(n=512):
        return R(ring("f"), 0, n)

    def PB():
        pr[0] += 1
        return "p%d" % pools[pool[0]][pr[0] % len(pools[pool[0]])]

    def PQ(n=512):
        return R(PB(), 0, n)

    CH = [(512 * k, 512 * k + 512) for k in range(4)] + [(V, W)]
    LSB = {d: R("ls", 8 * (d - 1), 8 * d) for d in (1, 2, 3)}
    LSA = R("ls", 0, 24)
    THR = R("th32", 0, 1)
    XA, KEY = R("xa", 0, W), R("key", 0, W)
    ONE = R("one", 0, 512)

    def M(name):
        return R(name, 0, 128)

    def shifted(name, k):
        return R(name, 16 - k, 144 - k)

    def lists(wf, ln):
        pb = PQ(304)
        for h in (0, 1):
            mm(R(pb[0], 152 * h, 152 * h + 152), [(M("pm%d%d" % (h, c)), R(wf, c, 304, 2)) for c in (0, 1)])
        vts(R(ln, 0, 304), pb, MG, OP.add, -MG, OP.add)

    def wrap(flat, wf, lp, ln, rows="wz"):
        pb = PQ(304)
        mm(pb, [(shifted(rows, i), R(flat, i, P2, 16)) for i in range(16)])
        sact(R(wf, 0, 304), pb, AF.Identity, bias=-0.5)
        vcopy(R(lp, 0, 304), pb)
        lists(wf, ln)

    def partners(wf, dn, dp):
        pb = PQ(256)
        mm(pb, [(M("swp"), R(wf, 0, 256))])
        vtt(R(dn, 0, 256), pb, R(wf, 0, 256), OP.subtract)
        vtt(R(dp, 0, 256), R(wf, 0, 256), R("pih", 0, 256), OP.subtract)

    def lst(l, c, h, k):
        return R("l%d%s" % (l, c), 152 * h + CH[k][0] // 16, 152 * h + CH[k][1] // 16)

    def pc(n, h, k):
        a, b = CH[k]
        o = V * h if k < 4 else V + GH * h
        return R(n, o + a, o + b)

    def chain(l, k, win, f, q, bias=0.0):
        lin(q, IND(win, lst(l, "n", 0, k)), bias=bias)
        for c, h in (("n", 1), ("p", 0), ("p", 1)):
            vtt(q, IND(win, lst(l, c, h, k)), q, f)

    for k in range(2):
        dma(T.x0i[:, 1024 * k:1024 * k + 1024], T.x0[:, 1024 * k:1024 * k + 1024], [R("x0i", 1024 * k, 1024 * k + 1024)], [])
    dma(T.x0i[:, 2352:2376], T.shw[:], [R("x0i", 2352, 2376)], [])
    dma(T.x0i[:, 2048:2352], T.nxt[:], [R("x0i", 2048, 2352)], [])
    dma(T.x0i[:, 2376:2377], T.th[:], [R("x0i", 2376, 2377)], [])
    iota(R("pci", 0, 1), [[0, 1]], 0, 1)
    iota(R("t0", 0, 512), [[64, 8], [0, 64]], 0, 0)
    iota(R("t1", 0, 512), [[0, 8], [1, 64]], 0, 0)
    vset(ONE, 1.0)
    for n in ("blk", "sel", "seq"):
        vset(M(n), 1.0)
    vset(M("hlf"), 0.5)
    vset(R("un", 0, 2052), 0.0)
    for n in ("wz", "wq", "rz", "rn"):
        vset(R(n, 0, 144), 0.0)
    for n, lo, hi in (("sel", 0, 1), ("seq", 2, 3), ("blk", 0, 15)):
        asel(M(n), M(n), [[-16, 8], [0, 16]], OP.is_ge, -lo, 1)
        asel(M(n), M(n), [[16, 8], [0, 16]], OP.is_ge, hi, -1)
    asel(M("idn"), R("one", 0, 128), [[-1, 128]], OP.is_equal, 0, 1)
    for h in (0, 1):
        for c in (0, 1):
            asel(M("pm%d%d" % (h, c)), M("hlf"), [[-16, 8], [1000, 2], [-2, 8]], OP.is_equal, -h - 1000 * c, 1)
    vts(R("pci", 1, 2), R("pci", 0, 1), 1, OP.bitwise_and)
    vts(R("pci", 2, 3), R("pci", 0, 1), 15, OP.bitwise_and)
    vcopy(R("col", 0, 1), R("pci", 1, 2))
    vts(R("col", 1, 2), R("col", 0, 1), -1.0, OP.mult, 1.0, OP.add)
    vcopy(R("col", 2, 3), R("pci", 2, 3))
    for b in range(1, 10):
        vts(R("col", 2 + b, 3 + b), R("col", 1, 2), 512.0 * b, OP.mult)
    vts(R("t2", 0, 512), R("t0", 0, 512), R("col", 1, 2), OP.mult)
    vts(R("t3", 0, 512), R("t1", 0, 512), R("col", 0, 1), OP.mult)
    vtt(R("phl", 0, 512), R("t2", 0, 512), R("t3", 0, 512), OP.add)
    first[0] = 100.0
    vcopy(R("ls", 0, 24), R("x0i", 2352, 2376))
    for k in range(2):
        vcopy(R("xa", 1024 * k, 1024 * k + 1024), R("x0i", 1024 * k, 1024 * k + 1024))
    sact(R("bs", 0, GH), IND(R("xa", 0, V), LSA))
    send(peers, [("bs", 0, "xa", V)], "ax1_", [R("bs", 0, GH)])
    recv("ax1_", homes, [("xa", V)])
    first[0] = 0.0
    vcopy(R("nxf", 0, 304), R("x0i", 2048, 2352))
    vts(R("nxf", 0, 304), R("nxf", 0, 304), -0.5, OP.add)
    vcopy(R("lpn", 0, 304), R("x0i", 2048, 2352))
    for b in range(1, 10):
        n = min(512, P2 - 512 * b)
        sact(R("phl", 512 * b, 512 * b + n), R("phl", 0, n), AF.Identity, bias=R("col", 2 + b, 3 + b))
    lists("nxf", "l1n")
    vcopy(IND(R("pvh", 0, P2), R("lpn", 0, 256)), R("phl", 0, 4096))
    vcopy(IND(R("pvh", 0, P2), R("lpn", 256, 304)), R("phl", 4096, P2))
    vset(M("swp"), 1.0)
    vset(M("qr"), 3.0 / 1024.0)
    vset(M("mgc"), MG / 128.0)
    vset(R("nm", 0, V), 0.0)
    for d in (1, 2, 3):
        vcopy(IND(R("nm", 0, V), LSB[d]), R("one", 0, 128))
    vcopy(THR, R("x0i", 2376, 2377))
    for n, i, c in (("neg", "idn", -1.0), ("ngq", "idn", -0.25), ("d25", "idn", 33554432.0), ("blp", "blk", 4096.0),
                    ("bln", "blk", -4096.0)):
        sact(M(n), M(i), scale=c)
    sact(R("ghl", 0, 768), R("phl", 4096, P2))
    sact(R("wz", 16, 144, 16), R("sel", 0, 128, 16))
    sact(R("wq", 16, 144, 16), R("seq", 0, 128, 16))
    for h in (0, 1):
        sact(R("rz", 16 + h, 144, 16), R("blk", h, 128, 16))
        sact(R("rn", 16 + h, 144, 16), R("blk", h, 128, 16), scale=-1.0)
    asel(R("un", 4, 2052, 4), ONE, [[-1, 16], [-16, 8], [0, 4]], OP.is_equal, 0, 1)
    asel(R("swp", 0, 128, 2), R("swp", 0, 128, 2), [[-2, 64]], OP.is_equal, -1, 1)
    asel(R("swp", 1, 128, 2), R("swp", 1, 128, 2), [[-2, 64]], OP.is_equal, 0, 1)
    iota(R("pid", 0, 304), [[16, 304]], 0, 0)
    vts(R("pid", 0, 304), R("pid", 0, 304), R("col", 2, 3), OP.add)
    vts(R("pih", 0, 256), R("pid", 0, 256), -0.5, OP.add)
    vcopy(M("idh"), M("idn"))
    vcopy(M("neh"), M("neg"))
    vcopy(M("nqh"), M("ngq"))

    for k in range(5):
        for h in (0, 1):
            lin(pc("fnx", h, k), IND(XA, lst(1, "n", h, k)))
    wrap("pvh", "pvf", "lpp", "l1p")
    partners("nxf", "dnn", "dpn")
    partners("pvf", "dnp", "dpp")

    for l in (1, 2, 3):
        LVn = "lv%d" % l
        srcs = {1: [("fpv", "fnx")], 2: [("ga", "gb")], 3: [("fpv", "fnx"), ("pvh", "nxh")]}[l]
        I1, NI, NQ = [M(x) for x in (("idh", "neh", "nqh") if l == 2 else ("idn", "neg", "ngq"))]
        pool[0] = "a"
        zb, tk = {}, {}

        def gathers(k):
            a, b = CH[k]
            n = b - a
            fp, fn = srcs[0]
            if l > 1:
                for h in (0, 1):
                    lin(pc(fn, h, k), IND(XA, lst(l, "n", h, k)))
            for h in (0, 1):
                lin(pc(fp, h, k), IND(XA, lst(l, "p", h, k)))
            if l == 3:
                for s, c in (("nxh", "n"), ("pvh", "p")):
                    for h in (0, 1):
                        lin(pc(s, h, k), IND(R("phl", W, P2), lst(l, c, h, k)), bias=-0.375)
            zb[k] = R("p%d" % (4 + k), 0, 512) if k < 4 else PQ(n)
            one = R("one", 0, n)
            mm(zb[k], [(NQ, pc(p[1], h, k)) for p in srcs for h in (0, 1)] + ([(M("qr"), one)] if l < 3 else []), stop=False)
            mm(zb[k], [(NQ, pc(p[0], h, k)) for p in srcs for h in (0, 1)] + [(M("mgc"), one)], start=False)
            xm = F(n)
            lin(xm, R("xa", a, b), bias=-MG)
            vtt(zb[k], zb[k], xm, OP.add)

        def sized(k):
            return [(M("sel"), R("phl", CH[k][0], CH[k][1])), (M("blp" if l == 1 else "bln"), tk[k])]

        def detail(k):
            a, b = CH[k]
            n, d = b - a, zb[k]
            t = e = tk[k] = R("tk", a, b) if k < 4 else R(ring("t"), 0, n)
            if l == 1:
                sact(t, d, AF.Abs)
            else:
                e = F(n)
                sact(e, d, AF.Abs)
                sact(t, e, AF.Relu, bias=255.0, scale=-1.0)
            o = PQ(n)
            mm(o, sized(k))
            lin(R("key", a, b), o)
            if k == 4:
                return
            m, w, q, ds = R(ring("m"), 0, 512), F(), F(), PQ()
            vts(m, e, THR, OP.is_ge)
            if l < 3:
                lin(w, m, bias=KP)
            else:
                lin(w, m, -1.0, 1.0)
            lin(q, d, 0.25, -0.375)
            vtt(R("dd", a, b), d, m, OP.mult)
            vts(ds, q, MG, OP.add, -MG, OP.add)
            vtt(d, ds, w, OP.mult)

        def chosen(k):
            a, b = CH[k]
            f = R(ring("q"), 0, 512)
            chain(l, k, KEY, OP.min, f)
            o = PQ()
            mm(o, [(M("d25"), R(x, a, b)) for x in ["nm"] + ["lv%d" % j for j in range(1, l)]] + sized(k))
            vtt(R(LVn, a, b), o, f, OP.is_lt)

        def likeness(k):
            terms = []
            for x, y in ((0, 0), (1, 1), (0, 1), (1, 0)):
                u = PQ()
                mm(u, [(I1, pc(s[0], x, k)) for s in srcs] + [(NI, pc(s[1], y, k)) for s in srcs])
                tn = ring("t")
                if l == 1:
                    lin(R(tn, 0, 512), u, relu=True)
                else:
                    sact(R(tn, 0, 512), u, AF.Abs)
                    sact(R(tn, 0, 512), R(tn, 0, 512), AF.Relu, bias=255.0, scale=-1.0)
                sg = "rz" if (x == y) == (l == 1) else "rn"
                terms += [(shifted(sg, 2 * i), R(tn, i, 512, 8)) for i in range(8)]
            mm(R("p3", 64 * k, 64 * k + 64), terms)

        def links_small():
            lb = PB()
            for k in range(4):
                a, b = CH[k]
                mm(R(lb, 64 * k, 64 * k + 64), [(shifted("rz", 2 * i), R(LVn, a + i, b, 8)) for i in range(8)])
            lin(R("lw", 0, 256), R(lb, 0, 256), 1.0 / 16)
            vts(R("lc", 0, 256), R("p3", 0, 256), 0.0, OP.is_gt)
            vtt(R("lc", 0, 256), R("lc", 0, 256), R("lw", 0, 256), OP.mult)
            for (dn, dp, h, lo) in (("dnn", "dpn", "hn", "ln_"), ("dnp", "dpp", "hp", "lp_"))[:2 if l < 3 else 1]:
                vtt(R("w0", 0, 256), R("lc", 0, 256), R(dn, 0, 256), OP.mult)
                vtt(R("w1", 0, 256), R("lw", 0, 256), R(dp, 0, 256), OP.mult)
                vtt(R("w0", 0, 256), R("w0", 0, 256), R("w1", 0, 256), OP.add)
                vtt(R("w0", 0, 256), R("w0", 0, 256), R("pid", 0, 256), OP.add)
                lin(R(h, 0, 256), R("w0", 0, 256))
                vtt(R(lo, 0, 256), R("w0", 0, 256), R(h, 0, 256), OP.subtract)

        def unwrap():
            if l != 2:
                lin(R("fnx", 4096, P2), R("ghl", 0, 768))
            for i in range(16):
                if i % 2 == 0:
                    bn = PB()
                bk = R(bn, 256 * (i % 2), 256 * (i % 2) + 256)
                mm(bk, [(R("un", 4 + 128 * i - r, 132 + 128 * i - r), R(x, 0, 256))
                        for r, x in enumerate(("hn", "ln_", "hp", "lp_")[:4 if l < 3 else 2])])
                lin(R("fnx", i, 4096, 16), bk)

        def own(k):
            a, b = CH[k]
            x, b1, b2 = R("xa", a, b), PQ(), PQ()
            if l < 3:
                s = R("sp%d" % l, a, b)
                chain(l, k, KEY, OP.add, s)
                z = F()
                lin(z, s, bias=MG * KP)
                lin(b1, z, 1.0 / KP, -MG)
                lin(b2, z, bias=-MG * KP)
                vtt(x, b1, x, OP.add)
                vtt(s, s, b2, OP.subtract)
            else:
                q = R(ring("q"), 0, 512)
                lin(b2, R(LVn, a, b), -BIG)
                vtt(x, b2, x, OP.add)
                chain(l, k, KEY, OP.add, q)
                vtt(x, q, x, OP.add)

        def border(buf, rc):
            for d in (1, 2, 3):
                c = rc + (d - 1) * B
                vtt(R("bt", 0, 128), IND(R(buf, 0, V), LSB[d]), R(rs, c, c + B), OP.add)
                vcopy(IND(R(buf, 0, V), LSB[d]), R("bt", 0, 128))

        def kept(k):
            a, b = CH[k]
            b2 = PQ()
            lin(b2, R(LVn, a, b), BIG, -(BIG + MG))
            vtt(R("dd" if l == 3 else "dl%d" % l, a, b), b2, R("dd", a, b), OP.add)
            if l < 3:
                b1, s = PQ(), R("sp%d" % l, a, b)
                lin(b1, R(LVn, a, b), BIG)
                vtt(s, b1, s, OP.add)

        if l == 3:
            for k in range(5):
                a, b = CH[k]
                t = R(ring("t"), 0, b - a)
                lin(t, R("xa", a, b))
                vtt(R("phl", W + a, W + b), R("xa", a, b), t, OP.subtract)
        order = [4, 0, 1, 2, 3] if l > 1 else [0, 1, 2, 3, 4]
        for i in range(6):
            if i < 5:
                gathers(order[i])
            if i > 0:
                detail(order[i - 1])
        for k in range(4):
            chosen(k)
            if k < (4 if l < 3 else 2):
                likeness(k)
        vset(R("key", V, W), 0.0)
        for k in range(4):
            a, b = CH[k]
            vtt(R("key", a, b), zb[k], R(LVn, a, b), OP.mult)
        pool[0] = "c"
        rs = "rs2" if l == 2 else "rs1"
        xg = [R("xa", V, W)]
        if l < 3:
            q, z, b4 = F(GH), F(GH), PQ(GH)
            chain(l, 4, KEY, OP.add, q)
            lin(z, q, bias=MG * KP)
            lin(b4, z, bias=-MG * KP)
            lin(R("ss", 0, GH), z, 1.0 / KP, -MG)
            vtt(R("ss", GH, 768), q, b4, OP.subtract)
            send(homes, [("ss", 0, rs, 0), ("ss", GH, rs, GH)], "as%d_" % l, [R("ss", 0, 768)], xg)
            recv("as%d_" % l, peers, [(rs, 0), (rs, GH)])
            links_small()
            own(0)
            own(1)
            unwrap()
            own(2)
            own(3)
            border("xa", 0)
            sact(R("bs", 0, GH), IND(R("xa", 0, V), LSA))
            send(peers, [("bs", 0, "xa", V)], "ax%d_" % (l + 1), [R("bs", 0, GH)], [R("rs1", 0, 768)] if l == 2 else [])
            recv("ax%d_" % (l + 1), homes, [("xa", V)])
            for (o, lp) in (("nxh", "lpn"), ("pvh", "lpp")):
                for k in range(4):
                    lin(R(o, 1216 * k, 1216 * k + 1216), IND(R("fnx", 0, P2), R(lp, 76 * k, 76 * k + 76)))
            wrap("nxh", "nxf", "lpn", "l%dn" % (l + 1))
            border("sp%d" % l, GH)
            sact(R("sg%d" % l, 0, GH), IND(R("sp%d" % l, 0, V), LSA))
            for k in range(4):
                kept(k)
            wrap("pvh", "pvf", "lpp", "l%dp" % (l + 1), "wq")
            partners("nxf", "dnn", "dpn")
            if l < 2:
                partners("pvf", "dnp", "dpp")
        else:
            chain(l, 4, KEY, OP.add, R("ss", 0, GH))
            send(homes, [("ss", 0, rs, 0)], "as3_", [R("ss", 0, GH)], xg)
            recv("as3_", peers, [(rs, 0)])
            for k in range(4):
                own(k)
            border("xa", 0)
            sact(R("bs", 0, GH), IND(R("xa", 0, V), LSA))
            vtt(R("bs", GH, 2 * GH), R("bs", 0, GH), R("sg2", 0, GH), OP.subtract)
            vtt(R("bs", 2 * GH, 3 * GH), R("bs", GH, 2 * GH), R("sg1", 0, GH), OP.subtract)
            send(peers, [("bs", 0, "xa", V)], "ab3_", [R("bs", 0, GH)])
            send(peers, [("bs", GH, "rb2", 0), ("bs", 2 * GH, "rb1", 0)], "ab2_", [R("bs", GH, 3 * GH)])
            recv("ab3_", homes, [("xa", V)])
            recv("ab2_", homes, [("rb2", 0), ("rb1", 0)])
            for k in range(4):
                kept(k)
            sact(R("key", V, W), R("rb2", 0, GH))
            likeness(2)
            likeness(3)
            links_small()
            unwrap()

    pool[0] = "z"

    def undo(l, src, dst, dl, sp):
        fms = {}
        for k in range(5):
            if k < 4:
                z, fms[k] = R(ring("q"), 0, 512), PQ()
                chain(l, k, R(src, 0, W), OP.add, z, -1.5)
                lin(fms[k], z, 0.25, MG)
            if k > 0:
                a, b = CH[k - 1]
                y, mx = PQ(), PQ()
                vtt(y, fms[k - 1], R(dl, a, b), OP.add)
                if sp is None:
                    vtt(R(dst, a, b), y, R(src, a, b), OP.max)
                    dma(T.yx[:, a:b], T[dst][:, a:b], [], [R(dst, a, b)])
                else:
                    vtt(mx, y, R(src, a, b), OP.max)
                    vtt(R(dst, a, b), mx, R(sp, a, b), OP.subtract)

    undo(3, "xa", "key", "dd", "sp2")
    sact(R("xa", V, W), R("rb1", 0, GH))
    for k in range(4):
        lin(R("nxh", 1216 * k, 1216 * k + 1216), IND(R("fnx", 0, P2), R("lpn", 76 * k, 76 * k + 76)))
    undo(2, "key", "xa", "dl2", "sp1")
    for k in range(10):
        a, b = 512 * k, min(512 * k + 512, P2)
        bk = PQ(b - a)
        mm(bk, [(M("sel"), R("nxh", a, b))])
        o = R("dd", a, b) if k < 4 else R("sp2", a - V, b - V) if k < 8 else R("f%d" % (k - 8), 0, b - a)
        lin(o, bk)
        if k == 3 or k == 7:
            nm = "dd" if k == 3 else "sp2"
            dma(T.yn[:, b - V:b], T[nm][0:128:16, 0:V], [], [R(nm, 0, V)])
        if k >= 8:
            dma(T.yn[:, a:b], T[o[0]][0:128:16, 0:b - a], [], [o])
    undo(1, "xa", "key", "dl1", None)

    for emit in ordered(prog):
        emit()

    for e in ("v", "s", "t", "g"):
        g.wait_ge(T.sem[semof[e]], tick[e])
    for k in range(ndma[0]):
        g.wait_ge(T.sem["d%d" % k], 16)
    for s, n in arrived.items():
        g.wait_ge(T.sem[s], n)
    g.wait_ge(T.sem["loc"], local[0])
